import numpy as np
import ml_dtypes


def mxq(x, axis, fmt="e4m3"):
    dtype, down = {"e4m3": (ml_dtypes.float8_e4m3fn, 7), "e5m2": (ml_dtypes.float8_e5m2, 14)}[fmt]
    v = np.moveaxis(np.asarray(x, np.float32).astype(ml_dtypes.bfloat16).astype(np.float64), axis, -1)
    blocks = v.reshape(v.shape[:-1] + (-1, 32))
    amax = np.abs(blocks).max(-1, keepdims=True)
    byte = np.maximum(np.where(amax > 0, np.frexp(amax)[1] - 1 + 127, 0) - down, 1)
    scale = np.exp2(byte - 127.0)
    codes = (blocks / scale).astype(np.float32).astype(dtype).astype(np.float64)
    return np.moveaxis((codes * scale).reshape(v.shape), -1, axis)


WIDE = False


def mx_kscale(k):
    if not WIDE:
        return np.ones(k)
    levels = np.array([10, -10, 5, -5, 0])
    if k % 512:
        return np.exp2(np.random.permutation(np.resize(levels, k // 32))).repeat(32)
    a = np.empty((k // 512, 16))
    for p in range(k // 512):
        a[p, :8] = np.random.permutation(np.resize(levels, 8))
        for g in range(8):
            far = levels[np.abs(levels - a[p, g]) >= 10]
            a[p, g + 8] = far[np.random.randint(len(far))]
    return np.exp2(a.ravel()).repeat(32)


def f64(x):
    return np.asarray(x).astype(np.float64)


def striped(idx):
    return np.tile(idx.reshape(-1, 16).T, (8, 1)).astype(np.uint16)


def unstriped(offs):
    return offs[:16].T.reshape(-1).astype(np.int64)


E2M1 = np.array([0.0, 0.5, 1.0, 1.5, 2.0, 3.0, 4.0, 6.0, -0.0, -0.5, -1.0, -1.5, -2.0, -3.0, -4.0, -6.0])


def pack_weight(w, fmt):
    k, n = w.shape
    w = f64(np.asarray(w, np.float32).astype(ml_dtypes.bfloat16)).reshape(k // 32, 32, n)
    amax = np.abs(w).max(1)
    if fmt == "e4m3":
        byte = np.frexp(amax)[1] - 1 + 127 - 7
    else:
        mant, ex = np.frexp(amax / 6.0)
        byte = np.where(mant > 0.5, ex, ex - 1) + 127
    byte = np.clip(np.where(amax > 0, byte, 1), 1, 254)
    scaled = (w * np.exp2(127.0 - byte)[:, None, :]).reshape(k, n).astype(np.float32)
    by_word = np.ascontiguousarray(scaled.reshape(k // 512, 128, 4, n).transpose(0, 1, 3, 2))
    if fmt == "e4m3":
        words = by_word.astype(ml_dtypes.float8_e4m3fn).view(np.uint8)
    else:
        c = by_word.astype(ml_dtypes.float4_e2m1fn).view(np.uint8) & 0xF
        words = (c[..., 0::2] | (c[..., 1::2] << 4)).reshape(k // 512, 128, 2 * n)
    return np.ascontiguousarray(words), np.ascontiguousarray(byte.astype(np.uint8).reshape(k // 512, 16, n))


def unpack_weight(words, scales, fmt):
    g, _, n = scales.shape
    words = np.ascontiguousarray(words).reshape(g, 128, n, -1)
    if fmt == "e4m3":
        vals = words.view(ml_dtypes.float8_e4m3fn).astype(np.float64)
    else:
        nib = np.empty((g, 128, n, 4), np.uint8)
        nib[..., 0::2] = words & 0xF
        nib[..., 1::2] = words >> 4
        vals = E2M1[nib]
    vals = vals * np.repeat(np.exp2(scales.astype(np.float64) - 127.0), 8, axis=1)[..., None]
    return vals.transpose(0, 1, 3, 2).reshape(g * 512, n)


def gelu(v):
    return 0.5 * v * (1.0 + np.tanh(np.sqrt(2.0 / np.pi) * (v + 0.044715 * v**3)))


K, T, E, C, H, N = 512, 640, 6, 128, 512, 384
TOP = 4
PAD = 64


def by_expert(wq, xq):
    return np.concatenate([wq[e].T @ xq[:, e * C:(e + 1) * C] for e in range(E)], axis=1)


def setup_inputs():
    n = np.random.standard_normal
    s = mx_kscale(K)[:, None]
    u = mx_kscale(H)
    slot_token = np.empty(E * C, np.int64); pos = np.tile(E * C + np.arange(T) % PAD, (TOP, 1)); taken = np.zeros(T, np.int64)
    liked = np.random.randn(T)
    for e in np.random.permutation(E):
        free = np.flatnonzero(taken < TOP); pick = np.random.permutation(free[np.argsort(-(liked[free] + np.random.gumbel(size=free.size)))[:C]]); slot_token[e * C:(e + 1) * C] = pick
        pos[taken[pick], pick] = e * C + np.arange(C); taken[pick] += 1
    g = np.random.uniform(0.2, 0.8, (TOP, T))
    w1 = [pack_weight(m, "e2m1") for m in n((E, K, H)) / np.sqrt(K) / s[None]]
    w3 = [pack_weight(m, "e2m1") for m in n((E, K, H)) / np.sqrt(K) / s[None] * u[None, None, :]]
    w2 = [pack_weight(m, "e2m1") for m in n((E, H, N)) / np.sqrt(H) / u[None, :, None]]
    x = pack_weight(n((K, T)) * s, "e4m3")
    return {
        "x_words": x[0],
        "x_scales": x[1],
        "w1_words": np.stack([m[0] for m in w1]),
        "w1_scales": np.stack([m[1] for m in w1]),
        "w3_words": np.stack([m[0] for m in w3]),
        "w3_scales": np.stack([m[1] for m in w3]),
        "w2_words": np.stack([m[0] for m in w2]),
        "w2_scales": np.stack([m[1] for m in w2]),
        "gate": np.stack([np.tile(r, (N, 1)) for r in g]).astype(np.float32),
        "offs": striped(slot_token),
        "pos1": striped(pos[0]),
        "pos2": striped(pos[1]),
        "pos3": striped(pos[2]),
        "pos4": striped(pos[3]),
    }


def reference(x_words, x_scales, w1_words, w1_scales, w3_words, w3_scales, w2_words, w2_scales, gate, offs, pos1, pos2, pos3, pos4):
    idx = unstriped(offs)
    w1 = np.stack([unpack_weight(w1_words[e], w1_scales[e], "e2m1") for e in range(E)])
    w3 = np.stack([unpack_weight(w3_words[e], w3_scales[e], "e2m1") for e in range(E)])
    w2 = np.stack([unpack_weight(w2_words[e], w2_scales[e], "e2m1") for e in range(E)])
    xq = unpack_weight(x_words, x_scales, "e4m3")[:, idx]
    h = gelu(by_expert(w1, xq))
    h = h * by_expert(w3, xq)
    y = by_expert(w2, mxq(h, 0, "e4m3"))
    y = np.concatenate([y, np.zeros((N, PAD))], axis=1)
    return sum(f64(gate[r]) * y[:, unstriped(p)] for r, p in enumerate((pos1, pos2, pos3, pos4)))

@@ -1,0 +1,220 @@
+from contextlib import ExitStack
+
+import concourse.mybir as mybir
+from concourse.masks import make_identity
+
+K, T, E, C, H, N = 512, 640, 6, 128, 512, 384
+TOP, PAD = 4, 64
+S = E * C
+P = 128
+NB = N // P
+TB = T // P
+BANK = 512
+
+F32 = mybir.dt.float32
+BF16 = mybir.dt.bfloat16
+I32 = mybir.dt.int32
+U32 = mybir.dt.uint32
+U16 = mybir.dt.uint16
+U8 = mybir.dt.uint8
+FP8X4 = mybir.dt.float8_e4m3fn_x4
+FP4X4 = mybir.dt.float4_e2m1fn_x4
+MULT = mybir.AluOpType.mult
+ADD = mybir.AluOpType.add
+GELU = mybir.ActivationFunctionType.Gelu_apprx_tanh
+
+FLOPS = 2 * S * (2 * K * H + H * N)
+BYTES = K * T + 16 * T + E * (2 * (K * H // 2 + 16 * H) + H * N // 2 + 16 * N) + 4 * TOP * T + 2 * P * (S + TOP * T) // 16 + 4 * N * T
+
+
+def tile_moe_ecr_glu_gelu_kernel(tc, x_words, x_scales, w1_words, w1_scales, w3_words, w3_scales, w2_words, w2_scales, gate, offs, pos1, pos2, pos3, pos4, out):
+    nc = tc.nc
+    with ExitStack() as ctx:
+        keep = ctx.enter_context(tc.tile_pool(name="keep", bufs=1))
+        psum = ctx.enter_context(tc.psum_pool(name="psum", bufs=1))
+
+        def sb(name, shape, dtype):
+            return keep.tile(shape, dtype, name=name, align_bytes=64)
+
+        def bank(b, name):
+            return psum.tile([P, BANK], F32, name=name, tag="bank%d" % b)
+
+        def zero_plane(engine, name, width):
+            plane = sb(name, [P, width], U8)
+            engine.memset(plane[:].bitcast(I32), 0)
+            return plane
+
+        xs = zero_plane(nc.vector, "xs", T)
+        w1s = zero_plane(nc.vector, "w1s", E * H)
+        w3s = zero_plane(nc.vector, "w3s", E * H)
+        w2s = zero_plane(nc.vector, "w2s", E * N)
+
+        def load_rows(plane, scales):
+            by_r = scales.rearrange("e (q r) c -> r q e c", r=4)
+            for r in range(4):
+                dst = plane[r:P:32, :].bitcast(I32).rearrange("q (e c) -> q e c", e=scales.shape[0])
+                nc.sync.dma_start(dst, by_r[r].bitcast(I32))
+
+        def load_words(name, words, e0, e1):
+            t = sb(name, [P, e1 - e0, words.shape[3]], U8)
+            nc.sync.dma_start(t[:].bitcast(I32), words.rearrange("e o p c -> p (e o) c")[:, e0:e1, :].bitcast(I32))
+            return t
+
+        xw = sb("xw", [P, T], I32)
+        nc.sync.dma_start(xw[:], x_words[0].rearrange("p t r -> p (t r)").bitcast(I32))
+        offs_sb = keep.tile([P, S // 16], U16, name="offs_sb")
+        nc.sync.dma_start(offs_sb[:], offs)
+        load_rows(xs, x_scales)
+        w1w, w3w = [], []
+        w1w.append(load_words("w1w0", w1_words, 0, 2))
+        load_rows(w1s, w1_scales.rearrange("e o q c -> (e o) q c"))
+        w3w.append(load_words("w3w0", w3_words, 0, 2))
+        load_rows(w3s, w3_scales.rearrange("e o q c -> (e o) q c"))
+        for g in (1, 2):
+            w1w.append(load_words("w1w%d" % g, w1_words, 2 * g, 2 * g + 2))
+            w3w.append(load_words("w3w%d" % g, w3_words, 2 * g, 2 * g + 2))
+        load_rows(w2s, w2_scales.rearrange("e o q c -> (e o) q c"))
+        w2w = load_words("w2w", w2_words, 0, E)
+        pos, gates = [], []
+        for r, lst in enumerate((pos1, pos2, pos3, pos4)):
+            t = keep.tile([P, T // 16], U16, name="pos_sb%d" % r)
+            nc.sync.dma_start(t[:], lst)
+            pos.append(t)
+        for r in range(TOP):
+            t = sb("gate%d" % r, [P, T], F32)
+            nc.sync.dma_start(t[:], gate[r, 0:P, :])
+            gates.append(t)
+
+        ident = sb("ident", [P, P], F32)
+        make_identity(nc, ident[:])
+        y = []
+        for nb in range(NB):
+            t = sb("y%d" % nb, [P, S + PAD], F32)
+            nc.gpsimd.memset(t[:, S:], 0.0)
+            y.append(t)
+
+        xg, xsg = [], []
+        for g in range(E // 2):
+            cols = offs_sb[:, 16 * g : 16 * g + 16]
+            tw = sb("xg%d" % g, [P, 2 * C], U32)
+            nc.vector.tensor_copy(tw[:], xw[:].bitcast(U32).indirect(cols))
+            ts = sb("xsg%d" % g, [P, 2 * C], U8)
+            nc.vector.tensor_copy(ts[:], xs[:].indirect(cols))
+            xg.append(tw)
+            xsg.append(ts)
+
+        a_ps, b_ps, act, ht, hq, hs = {}, {}, {}, {}, {}, {}
+
+        def first_layer(e):
+            g, j = divmod(e, 2)
+            cols = slice(j * C, (j + 1) * C)
+            a_ps[e] = bank(2 * (e % 3), "a%d" % e)
+            b_ps[e] = bank(2 * (e % 3) + 1, "b%d" % e)
+            for dst, words, plane in ((a_ps[e], w1w, w1s), (b_ps[e], w3w, w3s)):
+                nc.tensor.matmul_mx(
+                    dst[:],
+                    lhsT=xg[g][:, cols].bitcast(FP8X4),
+                    lhsT_scale=xsg[g][:, cols],
+                    rhs=words[g][:, j, :].bitcast(FP4X4),
+                    rhs_scale=plane[:, e * H : (e + 1) * H],
+                    start=True,
+                    stop=True,
+                )
+            act[e] = sb("act%d" % e, [P, 2, P, 2], F32)
+            nc.scalar.activation(act[e][:], a_ps[e][:].rearrange("s (p u d) -> s u p d", u=2, d=2), GELU)
+
+        def hidden(e):
+            h = sb("h%d" % e, [P, 2, P, 2], BF16)
+            nc.vector.tensor_tensor(h[:], b_ps[e][:].rearrange("s (p u d) -> s u p d", u=2, d=2), act[e][:], MULT)
+            pairs = h[:].rearrange("s u p d -> s (u p d)").bitcast(F32)
+            turned = bank(2 * (e % 3), "turned%d" % e)
+            for u in range(2):
+                nc.tensor.transpose(turned[:, u * P : (u + 1) * P], pairs[:, u * P : (u + 1) * P], ident[:])
+            ht[e] = sb("ht%d" % e, [P, 4 * C], BF16)
+            move = nc.vector.tensor_copy if e in (1, 3) else nc.scalar.copy
+            move(
+                ht[e][:].bitcast(F32).rearrange("p (s u) -> p s u", u=2),
+                turned[:, 0 : 2 * P].rearrange("p (u s) -> p s u", u=2),
+            )
+
+        def quantise(e):
+            hq[e] = sb("hq%d" % e, [P, C], U32)
+            hs[e] = sb("hs%d" % e, [P, C], U8)
+            nc.vector.quantize_mx(hq[e][:].bitcast(FP8X4), hs[e][:], ht[e][:])
+
+        def second_layer(dst, e, nb):
+            nc.tensor.matmul_mx(
+                dst,
+                lhsT=w2w[:, e, 2 * P * nb : 2 * P * (nb + 1)].bitcast(FP4X4),
+                lhsT_scale=w2s[:, e * N + P * nb : e * N + P * (nb + 1)],
+                rhs=hq[e][:].bitcast(FP8X4),
+                rhs_scale=hs[e][:],
+                start=True,
+                stop=True,
+            )
+
+        y_ps = None
+        for s in range(E + 3):
+            if 2 <= s <= E + 1:
+                hidden(s - 2)
+            if s < E:
+                first_layer(s)
+            if s >= 3:
+                e = s - 3
+                quantise(e)
+                if e in (0, 4, 5):
+                    y_ps = bank(6 if e == 0 else 7, "y0_%d" % e)
+                    first = e
+                second_layer(y_ps[:, (e - first) * C : (e - first + 1) * C], e, 0)
+                if e >= 3:
+                    nc.scalar.copy(y[0][:, first * C : (e + 1) * C], y_ps[:, 0 : (e + 1 - first) * C])
+
+        for nb, banks in ((2, (7, 6)), (1, (6, 7))):
+            for b, (e0, e1) in zip(banks, ((0, 4), (4, 6))):
+                y_ps = bank(b, "y%d_%d" % (nb, e0))
+                for e in range(e0, e1):
+                    second_layer(y_ps[:, (e - e0) * C : (e - e0 + 1) * C], e, nb)
+                nc.scalar.copy(y[nb][:, e0 * C : e1 * C], y_ps[:, 0 : (e1 - e0) * C])
+
+        def weighted(nb, r, t0, t1):
+            prod = sb("prod%d_%d_%d" % (nb, r, t0), [P, t1 - t0], F32)
+            nc.vector.tensor_tensor(prod[:], y[nb][:].indirect(pos[r][:, t0 // 16 : t1 // 16]), gates[r][:, t0:t1], MULT)
+            return prod
+
+        def summed(nb, terms, back_banks):
+            sums = [bank(tb, "sum%d_%d" % (nb, tb)) for tb in range(TB)]
+            for r in range(terms):
+                cuts = (0, 3, TB) if (nb, r) == (1, TOP - 1) else (0, TB)
+                for tb0, tb1 in zip(cuts, cuts[1:]):
+                    prod = weighted(nb, r, tb0 * P, tb1 * P)
+                    for tb in range(tb0, tb1):
+                        nc.tensor.matmul(
+                            sums[tb][:, 0:P], prod[:, (tb - tb0) * P : (tb - tb0 + 1) * P], ident[:],
+                            start=(r == 0), stop=(r == terms - 1), is_transpose=True,
+                        )
+            by_token = []
+            for tb in range(TB):
+                z = sb("z%d_%d" % (nb, tb), [P, P], F32)
+                nc.scalar.copy(z[:], sums[tb][:, 0:P])
+                by_token.append(z)
+            back = [bank(b, "back%d_%d" % (nb, b)) for b in back_banks]
+            for tb in range(TB):
+                nc.tensor.transpose(back[tb // 4][:, (tb % 4) * P : (tb % 4 + 1) * P], by_token[tb][:], ident[:])
+            return back
+
+        pieces = ((0, BANK), (BANK, T))
+
+        def store_sum(nb, back):
+            for (t0, t1), part in zip(pieces, back):
+                res = sb("res%d_%d" % (nb, t0), [P, t1 - t0], F32)
+                nc.scalar.copy(res[:], part[:, 0 : t1 - t0])
+                nc.sync.dma_start(out[nb * P : (nb + 1) * P, t0:t1], res[:])
+
+        store_sum(0, summed(0, TOP, (5, 6)))
+        partial = summed(2, TOP - 1, (7, 6))
+        store_sum(1, summed(1, TOP, (5, 0)))
+        last = [weighted(2, TOP - 1, t0, t1) for t0, t1 in pieces]
+        for (t0, t1), prod, part in zip(pieces, last, partial):
+            res = sb("res2_%d" % t0, [P, t1 - t0], F32)
+            nc.vector.tensor_tensor(res[:], part[:, 0 : t1 - t0], prod[:], ADD)
+            nc.sync.dma_start(out[2 * P : 3 * P, t0:t1], res[:])

@@ -10,6 +10,7 @@ P = 128
 NB = N // P
 TB = T // P
 BANK = 512
+WARM_PASSES = 10
 
 F32 = mybir.dt.float32
 BF16 = mybir.dt.bfloat16
@@ -44,46 +45,50 @@ def tile_moe_ecr_glu_gelu_kernel(tc, x_words, x_scales, w1_words, w1_scales, w3_
             engine.memset(plane[:].bitcast(I32), 0)
             return plane
 
-        xs = zero_plane(nc.vector, "xs", T)
+        xs = zero_plane(nc.gpsimd, "xs", T)
         w1s = zero_plane(nc.vector, "w1s", E * H)
         w3s = zero_plane(nc.vector, "w3s", E * H)
         w2s = zero_plane(nc.vector, "w2s", E * N)
 
-        def load_rows(plane, scales):
-            by_r = scales.rearrange("e (q r) c -> r q e c", r=4)
-            for r in range(4):
-                dst = plane[r:P:32, :].bitcast(I32).rearrange("q (e c) -> q e c", e=scales.shape[0])
-                nc.sync.dma_start(dst, by_r[r].bitcast(I32))
+        def load_row(plane, scales, r):
+            src = scales.rearrange("e (q r) c -> r q e c", r=4)[r]
+            dst = plane[r:P:32, :].bitcast(I32).rearrange("q (e c) -> q e c", e=scales.shape[0])
+            nc.sync.dma_start(dst, src.bitcast(I32))
 
-        def load_words(name, words, e0, e1):
-            t = sb(name, [P, e1 - e0, words.shape[3]], U8)
-            nc.sync.dma_start(t[:].bitcast(I32), words.rearrange("e o p c -> p (e o) c")[:, e0:e1, :].bitcast(I32))
+        def load_words(name, words, e0, e1, c0, c1):
+            t = sb(name, [P, e1 - e0, c1 - c0], U8)
+            nc.sync.dma_start(t[:].bitcast(I32), words.rearrange("e o p c -> p (e o) c")[:, e0:e1, c0:c1].bitcast(I32))
             return t
 
+        def load_list(name, lst):
+            t = keep.tile(list(lst.shape), U16, name=name)
+            nc.sync.dma_start(t[:], lst)
+            return t
+
+        w1_rows, w3_rows, w2_rows = (s.rearrange("e o q c -> (e o) q c") for s in (w1_scales, w3_scales, w2_scales))
         xw = sb("xw", [P, T], I32)
         nc.sync.dma_start(xw[:], x_words[0].rearrange("p t r -> p (t r)").bitcast(I32))
-        offs_sb = keep.tile([P, S // 16], U16, name="offs_sb")
-        nc.sync.dma_start(offs_sb[:], offs)
-        load_rows(xs, x_scales)
+        for r in range(4):
+            load_row(xs, x_scales, r)
+        offs_sb = load_list("offs_sb", offs)
         w1w, w3w = [], []
-        w1w.append(load_words("w1w0", w1_words, 0, 2))
-        load_rows(w1s, w1_scales.rearrange("e o q c -> (e o) q c"))
-        w3w.append(load_words("w3w0", w3_words, 0, 2))
-        load_rows(w3s, w3_scales.rearrange("e o q c -> (e o) q c"))
-        for g in (1, 2):
-            w1w.append(load_words("w1w%d" % g, w1_words, 2 * g, 2 * g + 2))
-            w3w.append(load_words("w3w%d" % g, w3_words, 2 * g, 2 * g + 2))
-        load_rows(w2s, w2_scales.rearrange("e o q c -> (e o) q c"))
-        w2w = load_words("w2w", w2_words, 0, E)
-        pos, gates = [], []
-        for r, lst in enumerate((pos1, pos2, pos3, pos4)):
-            t = keep.tile([P, T // 16], U16, name="pos_sb%d" % r)
-            nc.sync.dma_start(t[:], lst)
-            pos.append(t)
-        for r in range(TOP):
-            t = sb("gate%d" % r, [P, T], F32)
-            nc.sync.dma_start(t[:], gate[r, 0:P, :])
-            gates.append(t)
+        for g in range(E // 2):
+            w1w.append(load_words("w1w%d" % g, w1_words, 2 * g, 2 * g + 2, 0, 2 * H))
+            w3w.append(load_words("w3w%d" % g, w3_words, 2 * g, 2 * g + 2, 0, 2 * H))
+            if g == 0:
+                for r in range(3):
+                    load_row(w1s, w1_rows, r)
+                for r in range(3):
+                    load_row(w3s, w3_rows, r)
+                load_row(w1s, w1_rows, 3)
+                load_row(w3s, w3_rows, 3)
+        for r in range(4):
+            load_row(w2s, w2_rows, r)
+        w2_first = load_words("w2_first", w2_words, 0, E, 0, 2 * P)
+        pos = [load_list("pos_sb%d" % r, lst) for r, lst in enumerate((pos1, pos2, pos3, pos4))]
+        gates = sb("gates", [P, TOP, T], F32)
+        nc.sync.dma_start(gates[:], gate[:, 0:P, :].rearrange("r p t -> p r t"))
+        w2_rest = load_words("w2_rest", w2_words, 0, E, 2 * P, 2 * N)
 
         ident = sb("ident", [P, P], F32)
         make_identity(nc, ident[:])
@@ -93,104 +98,123 @@ def tile_moe_ecr_glu_gelu_kernel(tc, x_words, x_scales, w1_words, w1_scales, w3_
             nc.gpsimd.memset(t[:, S:], 0.0)
             y.append(t)
 
-        xg, xsg = [], []
-        for g in range(E // 2):
-            cols = offs_sb[:, 16 * g : 16 * g + 16]
-            tw = sb("xg%d" % g, [P, 2 * C], U32)
-            nc.vector.tensor_copy(tw[:], xw[:].bitcast(U32).indirect(cols))
-            ts = sb("xsg%d" % g, [P, 2 * C], U8)
-            nc.vector.tensor_copy(ts[:], xs[:].indirect(cols))
-            xg.append(tw)
-            xsg.append(ts)
+        xg, xsg = {}, {}
 
-        a_ps, b_ps, act, ht, hq, hs = {}, {}, {}, {}, {}, {}
+        def gather(into, name, window, dtype, e0, e1):
+            t = sb("%s%d" % (name, e0), [P, (e1 - e0) * C], dtype)
+            nc.vector.tensor_copy(t[:], window.indirect(offs_sb[:, e0 * C // 16 : e1 * C // 16]))
+            for e in range(e0, e1):
+                into[e] = t[:, (e - e0) * C : (e - e0 + 1) * C]
+
+        for e0, e1 in ((0, 1), (1, 3), (3, 6)):
+            gather(xg, "xg", xw[:].bitcast(U32), U32, e0, e1)
+            gather(xsg, "xsg", xs[:], U8, e0, e1)
+
+        a_ps, b_ps, act, hh, hq, hs = {}, {}, {}, {}, {}, {}
+        ht = sb("ht", [P, E * 4 * C], BF16)
+
+        warm = bank(5, "warm")
+        for i in range(WARM_PASSES):
+            nc.tensor.matmul_mx(
+                warm[:, (i % 4) * P : (i % 4 + 1) * P],
+                lhsT=xg[0].bitcast(FP8X4),
+                lhsT_scale=xsg[0],
+                rhs=w1w[0][:, 0, 0 : 2 * P].bitcast(FP4X4),
+                rhs_scale=xsg[0],
+                start=True,
+                stop=True,
+            )
 
         def first_layer(e):
             g, j = divmod(e, 2)
-            cols = slice(j * C, (j + 1) * C)
-            a_ps[e] = bank(2 * (e % 3), "a%d" % e)
-            b_ps[e] = bank(2 * (e % 3) + 1, "b%d" % e)
+            a_ps[e] = bank((0, 1, 7)[e % 3], "a%d" % e)
+            b_ps[e] = bank(2 + e % 3, "b%d" % e)
             for dst, words, plane in ((a_ps[e], w1w, w1s), (b_ps[e], w3w, w3s)):
                 nc.tensor.matmul_mx(
                     dst[:],
-                    lhsT=xg[g][:, cols].bitcast(FP8X4),
-                    lhsT_scale=xsg[g][:, cols],
+                    lhsT=xg[e].bitcast(FP8X4),
+                    lhsT_scale=xsg[e],
                     rhs=words[g][:, j, :].bitcast(FP4X4),
                     rhs_scale=plane[:, e * H : (e + 1) * H],
                     start=True,
                     stop=True,
                 )
-            act[e] = sb("act%d" % e, [P, 2, P, 2], F32)
+            tag = "shared" if e == E - 1 else "act%d" % e
+            act[e] = keep.tile([P, 2, P, 2], F32, name="act%d" % e, tag=tag, align_bytes=64)
             nc.scalar.activation(act[e][:], a_ps[e][:].rearrange("s (p u d) -> s u p d", u=2, d=2), GELU)
 
-        def hidden(e):
-            h = sb("h%d" % e, [P, 2, P, 2], BF16)
-            nc.vector.tensor_tensor(h[:], b_ps[e][:].rearrange("s (p u d) -> s u p d", u=2, d=2), act[e][:], MULT)
-            pairs = h[:].rearrange("s u p d -> s (u p d)").bitcast(F32)
-            turned = bank(2 * (e % 3), "turned%d" % e)
+        def product(e):
+            hh[e] = sb("h%d" % e, [P, 2, P, 2], BF16)
+            nc.vector.tensor_tensor(hh[e][:], b_ps[e][:].rearrange("s (p u d) -> s u p d", u=2, d=2), act[e][:], MULT)
+
+        def turn(e):
+            pairs = hh[e][:].rearrange("s u p d -> s (u p d)").bitcast(F32)
+            turned = bank(5 + e % 2, "turned%d" % e)
             for u in range(2):
                 nc.tensor.transpose(turned[:, u * P : (u + 1) * P], pairs[:, u * P : (u + 1) * P], ident[:])
-            ht[e] = sb("ht%d" % e, [P, 4 * C], BF16)
-            move = nc.vector.tensor_copy if e in (1, 3) else nc.scalar.copy
-            move(
-                ht[e][:].bitcast(F32).rearrange("p (s u) -> p s u", u=2),
+            nc.scalar.copy(
+                ht[:, e * 4 * C : (e + 1) * 4 * C].bitcast(F32).rearrange("p (s u) -> p s u", u=2),
                 turned[:, 0 : 2 * P].rearrange("p (u s) -> p s u", u=2),
             )
 
-        def quantise(e):
-            hq[e] = sb("hq%d" % e, [P, C], U32)
-            hs[e] = sb("hs%d" % e, [P, C], U8)
-            nc.vector.quantize_mx(hq[e][:].bitcast(FP8X4), hs[e][:], ht[e][:])
+        def quantise(e0, e1, tag):
+            codes = keep.tile([P, (e1 - e0) * C], U32, name="hq%d" % e0, tag=tag, align_bytes=64)
+            plane = sb("hs%d" % e0, [P, (e1 - e0) * C], U8)
+            nc.vector.quantize_mx(codes[:].bitcast(FP8X4), plane[:], ht[:, e0 * 4 * C : e1 * 4 * C])
+            for e in range(e0, e1):
+                hq[e] = codes[:, (e - e0) * C : (e - e0 + 1) * C]
+                hs[e] = plane[:, (e - e0) * C : (e - e0 + 1) * C]
 
         def second_layer(dst, e, nb):
             nc.tensor.matmul_mx(
                 dst,
-                lhsT=w2w[:, e, 2 * P * nb : 2 * P * (nb + 1)].bitcast(FP4X4),
+                lhsT=(w2_first[:, e, :] if nb == 0 else w2_rest[:, e, 2 * P * (nb - 1) : 2 * P * nb]).bitcast(FP4X4),
                 lhsT_scale=w2s[:, e * N + P * nb : e * N + P * (nb + 1)],
-                rhs=hq[e][:].bitcast(FP8X4),
-                rhs_scale=hs[e][:],
+                rhs=hq[e].bitcast(FP8X4),
+                rhs_scale=hs[e],
                 start=True,
                 stop=True,
             )
 
-        y_ps = None
         for s in range(E + 3):
-            if 2 <= s <= E + 1:
-                hidden(s - 2)
             if s < E:
                 first_layer(s)
+            if 2 <= s <= E + 1:
+                product(s - 2)
             if s >= 3:
-                e = s - 3
-                quantise(e)
-                if e in (0, 4, 5):
-                    y_ps = bank(6 if e == 0 else 7, "y0_%d" % e)
-                    first = e
-                second_layer(y_ps[:, (e - first) * C : (e - first + 1) * C], e, 0)
-                if e >= 3:
-                    nc.scalar.copy(y[0][:, first * C : (e + 1) * C], y_ps[:, 0 : (e + 1 - first) * C])
+                turn(s - 3)
+        quantise(0, 4, "shared")
+        quantise(4, 5, "hq4")
+        quantise(5, 6, "hq5")
 
-        for nb, banks in ((2, (7, 6)), (1, (6, 7))):
-            for b, (e0, e1) in zip(banks, ((0, 4), (4, 6))):
-                y_ps = bank(b, "y%d_%d" % (nb, e0))
-                for e in range(e0, e1):
-                    second_layer(y_ps[:, (e - e0) * C : (e - e0 + 1) * C], e, nb)
-                nc.scalar.copy(y[nb][:, e0 * C : e1 * C], y_ps[:, 0 : (e1 - e0) * C])
+        def results(nb, e0, e1, b, move=nc.scalar.copy):
+            y_ps = bank(b, "y%d_%d" % (nb, e0))
+            for e in range(e0, e1):
+                second_layer(y_ps[:, (e - e0) * C : (e - e0 + 1) * C], e, nb)
+            move(y[nb][:, e0 * C : e1 * C], y_ps[:, 0 : (e1 - e0) * C])
 
+        results(0, 0, 4, 3, nc.vector.tensor_copy)
+        results(0, 4, 5, 4)
+        results(0, 5, 6, 7)
+        results(2, 0, 4, 7)
+        results(2, 4, 6, 6)
+        results(1, 0, 4, 6)
+        results(1, 4, 6, 7)
         def weighted(nb, r, t0, t1):
             prod = sb("prod%d_%d_%d" % (nb, r, t0), [P, t1 - t0], F32)
-            nc.vector.tensor_tensor(prod[:], y[nb][:].indirect(pos[r][:, t0 // 16 : t1 // 16]), gates[r][:, t0:t1], MULT)
+            nc.vector.tensor_tensor(prod[:], y[nb][:].indirect(pos[r][:, t0 // 16 : t1 // 16]), gates[:, r, t0:t1], MULT)
             return prod
 
         def summed(nb, terms, back_banks):
             sums = [bank(tb, "sum%d_%d" % (nb, tb)) for tb in range(TB)]
-            for r in range(terms):
-                cuts = (0, 3, TB) if (nb, r) == (1, TOP - 1) else (0, TB)
+            for r in terms:
+                cuts = (0, 3, TB) if (nb, r) == (1, 0) else (0, TB)
                 for tb0, tb1 in zip(cuts, cuts[1:]):
                     prod = weighted(nb, r, tb0 * P, tb1 * P)
                     for tb in range(tb0, tb1):
                         nc.tensor.matmul(
                             sums[tb][:, 0:P], prod[:, (tb - tb0) * P : (tb - tb0 + 1) * P], ident[:],
-                            start=(r == 0), stop=(r == terms - 1), is_transpose=True,
+                            start=(r == terms[0]), stop=(r == terms[-1]), is_transpose=True,
                         )
             by_token = []
             for tb in range(TB):
@@ -210,10 +234,10 @@ def tile_moe_ecr_glu_gelu_kernel(tc, x_words, x_scales, w1_words, w1_scales, w3_
                 nc.scalar.copy(res[:], part[:, 0 : t1 - t0])
                 nc.sync.dma_start(out[nb * P : (nb + 1) * P, t0:t1], res[:])
 
-        store_sum(0, summed(0, TOP, (5, 6)))
-        partial = summed(2, TOP - 1, (7, 6))
-        store_sum(1, summed(1, TOP, (5, 0)))
-        last = [weighted(2, TOP - 1, t0, t1) for t0, t1 in pieces]
+        store_sum(0, summed(0, (3, 2, 1, 0), (5, 6)))
+        partial = summed(2, (3, 2, 1), (7, 6))
+        store_sum(1, summed(1, (3, 2, 1, 0), (5, 0)))
+        last = [weighted(2, 0, t0, t1) for t0, t1 in pieces]
         for (t0, t1), prod, part in zip(pieces, last, partial):
             res = sb("res2_%d" % t0, [P, t1 - t0], F32)
             nc.vector.tensor_tensor(res[:], part[:, 0 : t1 - t0], prod[:], ADD)

@@ -10,7 +10,10 @@ P = 128
 NB = N // P
 TB = T // P
 BANK = 512
-WARM_PASSES = 10
+WARM_PASSES = 8
+PAIR = 2
+A_BANKS = (0, 2, 4, 6, 0, 4)
+B_BANKS = (1, 3, 5, 7, 2, 6)
 
 F32 = mybir.dt.float32
 BF16 = mybir.dt.bfloat16
@@ -49,11 +52,13 @@ def tile_moe_ecr_glu_gelu_kernel(tc, x_words, x_scales, w1_words, w1_scales, w3_
         w1s = zero_plane(nc.vector, "w1s", E * H)
         w3s = zero_plane(nc.vector, "w3s", E * H)
         w2s = zero_plane(nc.vector, "w2s", E * N)
+        ident = sb("ident", [P, P], F32)
+        make_identity(nc, ident[:])
 
-        def load_row(plane, scales, r):
+        def load_row(queue, plane, scales, r):
             src = scales.rearrange("e (q r) c -> r q e c", r=4)[r]
             dst = plane[r:P:32, :].bitcast(I32).rearrange("q (e c) -> q e c", e=scales.shape[0])
-            nc.sync.dma_start(dst, src.bitcast(I32))
+            queue.dma_start(dst, src.bitcast(I32))
 
         def load_words(name, words, e0, e1, c0, c1):
             t = sb(name, [P, e1 - e0, c1 - c0], U8)
@@ -69,33 +74,34 @@ def tile_moe_ecr_glu_gelu_kernel(tc, x_words, x_scales, w1_words, w1_scales, w3_
         xw = sb("xw", [P, T], I32)
         nc.sync.dma_start(xw[:], x_words[0].rearrange("p t r -> p (t r)").bitcast(I32))
         for r in range(4):
-            load_row(xs, x_scales, r)
+            load_row(nc.sync, xs, x_scales, r)
         offs_sb = load_list("offs_sb", offs)
-        w1w, w3w = [], []
-        for g in range(E // 2):
-            w1w.append(load_words("w1w%d" % g, w1_words, 2 * g, 2 * g + 2, 0, 2 * H))
-            w3w.append(load_words("w3w%d" % g, w3_words, 2 * g, 2 * g + 2, 0, 2 * H))
-            if g == 0:
-                for r in range(3):
-                    load_row(w1s, w1_rows, r)
-                for r in range(3):
-                    load_row(w3s, w3_rows, r)
-                load_row(w1s, w1_rows, 3)
-                load_row(w3s, w3_rows, 3)
+        w1w = [load_words("w1w0", w1_words, 0, PAIR, 0, 2 * H)]
+        w3w = [load_words("w3w0", w3_words, 0, PAIR, 0, 2 * H)]
         for r in range(4):
-            load_row(w2s, w2_rows, r)
+            load_row(nc.sync if r < 3 else nc.gpsimd, w1s, w1_rows, r)
+        for r in range(4):
+            load_row(nc.sync if r < 3 else nc.gpsimd, w3s, w3_rows, r)
+        for r in range(2):
+            load_row(nc.gpsimd, w2s, w2_rows, r)
+        for g in range(1, E // PAIR):
+            w1w.append(load_words("w1w%d" % g, w1_words, PAIR * g, PAIR * (g + 1), 0, 2 * H))
+            w3w.append(load_words("w3w%d" % g, w3_words, PAIR * g, PAIR * (g + 1), 0, 2 * H))
         w2_first = load_words("w2_first", w2_words, 0, E, 0, 2 * P)
+        for r in range(2, 4):
+            load_row(nc.sync, w2s, w2_rows, r)
         pos = [load_list("pos_sb%d" % r, lst) for r, lst in enumerate((pos1, pos2, pos3, pos4))]
-        gates = sb("gates", [P, TOP, T], F32)
-        nc.sync.dma_start(gates[:], gate[:, 0:P, :].rearrange("r p t -> p r t"))
+        gates_rest = sb("gates_rest", [P, TOP - 1, T], F32)
+        nc.sync.dma_start(gates_rest[:], gate[1:TOP, 0:P, :].rearrange("r p t -> p r t"))
         w2_rest = load_words("w2_rest", w2_words, 0, E, 2 * P, 2 * N)
+        gate_first = sb("gate_first", [P, T], F32)
+        nc.sync.dma_start(gate_first[:], gate[0, 0:P, :])
+        gates = [gate_first[:]] + [gates_rest[:, r, :] for r in range(TOP - 1)]
 
-        ident = sb("ident", [P, P], F32)
-        make_identity(nc, ident[:])
         y = []
         for nb in range(NB):
             t = sb("y%d" % nb, [P, S + PAD], F32)
-            nc.gpsimd.memset(t[:, S:], 0.0)
+            nc.vector.memset(t[:, S:], 0.0)
             y.append(t)
 
         xg, xsg = {}, {}
@@ -113,7 +119,7 @@ def tile_moe_ecr_glu_gelu_kernel(tc, x_words, x_scales, w1_words, w1_scales, w3_
         a_ps, b_ps, act, hh, hq, hs = {}, {}, {}, {}, {}, {}
         ht = sb("ht", [P, E * 4 * C], BF16)
 
-        warm = bank(5, "warm")
+        warm = bank(7, "warm")
         for i in range(WARM_PASSES):
             nc.tensor.matmul_mx(
                 warm[:, (i % 4) * P : (i % 4 + 1) * P],
@@ -126,15 +132,15 @@ def tile_moe_ecr_glu_gelu_kernel(tc, x_words, x_scales, w1_words, w1_scales, w3_
             )
 
         def first_layer(e):
-            g, j = divmod(e, 2)
-            a_ps[e] = bank((0, 1, 7)[e % 3], "a%d" % e)
-            b_ps[e] = bank(2 + e % 3, "b%d" % e)
-            for dst, words, plane in ((a_ps[e], w1w, w1s), (b_ps[e], w3w, w3s)):
+            g, j = divmod(e, PAIR)
+            a_ps[e] = bank(A_BANKS[e], "a%d" % e)
+            b_ps[e] = bank(B_BANKS[e], "b%d" % e)
+            for dst, words, plane in ((a_ps[e], w1w[g][:, j, :], w1s), (b_ps[e], w3w[g][:, j, :], w3s)):
                 nc.tensor.matmul_mx(
                     dst[:],
                     lhsT=xg[e].bitcast(FP8X4),
                     lhsT_scale=xsg[e],
-                    rhs=words[g][:, j, :].bitcast(FP4X4),
+                    rhs=words.bitcast(FP4X4),
                     rhs_scale=plane[:, e * H : (e + 1) * H],
                     start=True,
                     stop=True,
@@ -144,17 +150,19 @@ def tile_moe_ecr_glu_gelu_kernel(tc, x_words, x_scales, w1_words, w1_scales, w3_
             nc.scalar.activation(act[e][:], a_ps[e][:].rearrange("s (p u d) -> s u p d", u=2, d=2), GELU)
 
         def product(e):
-            hh[e] = sb("h%d" % e, [P, 2, P, 2], BF16)
+            hh[e] = keep.tile([P, 2, P, 2], BF16, name="h%d" % e, tag="h%d" % e, align_bytes=64)
             nc.vector.tensor_tensor(hh[e][:], b_ps[e][:].rearrange("s (p u d) -> s u p d", u=2, d=2), act[e][:], MULT)
 
-        def turn(e):
-            pairs = hh[e][:].rearrange("s u p d -> s (u p d)").bitcast(F32)
-            turned = bank(5 + e % 2, "turned%d" % e)
-            for u in range(2):
-                nc.tensor.transpose(turned[:, u * P : (u + 1) * P], pairs[:, u * P : (u + 1) * P], ident[:])
-            nc.scalar.copy(
-                ht[:, e * 4 * C : (e + 1) * 4 * C].bitcast(F32).rearrange("p (s u) -> p s u", u=2),
-                turned[:, 0 : 2 * P].rearrange("p (u s) -> p s u", u=2),
+        def turn(e0, e1, b, move=nc.scalar.copy):
+            turned = bank(b, "turned%d" % e0)
+            for e in range(e0, e1):
+                pairs = hh[e][:].rearrange("s u p d -> s (u p d)").bitcast(F32)
+                for u in range(2):
+                    at = (2 * (e - e0) + u) * P
+                    nc.tensor.transpose(turned[:, at : at + P], pairs[:, u * P : (u + 1) * P], ident[:])
+            move(
+                ht[:, e0 * 4 * C : e1 * 4 * C].bitcast(F32).rearrange("p (e s u) -> p e s u", e=e1 - e0, u=2),
+                turned[:, 0 : 2 * P * (e1 - e0)].rearrange("p (e u s) -> p e s u", e=e1 - e0, u=2),
             )
 
         def quantise(e0, e1, tag):
@@ -176,14 +184,16 @@ def tile_moe_ecr_glu_gelu_kernel(tc, x_words, x_scales, w1_words, w1_scales, w3_
                 stop=True,
             )
 
-        for s in range(E + 3):
-            if s < E:
-                first_layer(s)
-            if 2 <= s <= E + 1:
-                product(s - 2)
-            if s >= 3:
-                turn(s - 3)
-        quantise(0, 4, "shared")
+        for e in range(E):
+            first_layer(e)
+        for e in range(E):
+            product(e)
+        turn(0, 2, A_BANKS[4])
+        turn(2, 4, B_BANKS[0])
+        turn(4, 5, B_BANKS[1])
+        turn(5, 6, B_BANKS[2])
+        quantise(0, 2, "shared")
+        quantise(2, 4, "hq2")
         quantise(4, 5, "hq4")
         quantise(5, 6, "hq5")
 
@@ -193,52 +203,74 @@ def tile_moe_ecr_glu_gelu_kernel(tc, x_words, x_scales, w1_words, w1_scales, w3_
                 second_layer(y_ps[:, (e - e0) * C : (e - e0 + 1) * C], e, nb)
             move(y[nb][:, e0 * C : e1 * C], y_ps[:, 0 : (e1 - e0) * C])
 
-        results(0, 0, 4, 3, nc.vector.tensor_copy)
-        results(0, 4, 5, 4)
-        results(0, 5, 6, 7)
-        results(2, 0, 4, 7)
+        results(0, 0, 2, 7, nc.vector.tensor_copy)
+        results(0, 2, 4, 4)
+        results(0, 4, 5, 2, nc.vector.tensor_copy)
+        results(0, 5, 6, 6)
+        results(2, 0, 4, 5)
         results(2, 4, 6, 6)
-        results(1, 0, 4, 6)
-        results(1, 4, 6, 7)
+        results(1, 0, 4, 7)
+        results(1, 4, 6, 6)
+
         def weighted(nb, r, t0, t1):
             prod = sb("prod%d_%d_%d" % (nb, r, t0), [P, t1 - t0], F32)
-            nc.vector.tensor_tensor(prod[:], y[nb][:].indirect(pos[r][:, t0 // 16 : t1 // 16]), gates[:, r, t0:t1], MULT)
+            nc.vector.tensor_tensor(prod[:], y[nb][:].indirect(pos[r][:, t0 // 16 : t1 // 16]), gates[r][:, t0:t1], MULT)
             return prod
 
-        def summed(nb, terms, back_banks):
-            sums = [bank(tb, "sum%d_%d" % (nb, tb)) for tb in range(TB)]
-            for r in terms:
-                cuts = (0, 3, TB) if (nb, r) == (1, 0) else (0, TB)
-                for tb0, tb1 in zip(cuts, cuts[1:]):
-                    prod = weighted(nb, r, tb0 * P, tb1 * P)
-                    for tb in range(tb0, tb1):
-                        nc.tensor.matmul(
-                            sums[tb][:, 0:P], prod[:, (tb - tb0) * P : (tb - tb0 + 1) * P], ident[:],
-                            start=(r == terms[0]), stop=(r == terms[-1]), is_transpose=True,
-                        )
+        def add_term(sums, nb, r, tb0, tb1, first, last):
+            prod = weighted(nb, r, tb0 * P, tb1 * P)
+            for tb in range(tb0, tb1):
+                nc.tensor.matmul(
+                    sums[tb][:, 0:P], prod[:, (tb - tb0) * P : (tb - tb0 + 1) * P], ident[:],
+                    start=first, stop=last(tb), is_transpose=True,
+                )
+
+        def turn_back(sums, nb, tb0, tb1, b):
             by_token = []
-            for tb in range(TB):
+            for tb in range(tb0, tb1):
                 z = sb("z%d_%d" % (nb, tb), [P, P], F32)
                 nc.scalar.copy(z[:], sums[tb][:, 0:P])
                 by_token.append(z)
-            back = [bank(b, "back%d_%d" % (nb, b)) for b in back_banks]
-            for tb in range(TB):
-                nc.tensor.transpose(back[tb // 4][:, (tb % 4) * P : (tb % 4 + 1) * P], by_token[tb][:], ident[:])
+            back = bank(b, "back%d_%d" % (nb, tb0))
+            for i, z in enumerate(by_token):
+                nc.tensor.transpose(back[:, i * P : (i + 1) * P], z[:], ident[:])
             return back
 
-        pieces = ((0, BANK), (BANK, T))
+        def store(back, nb, tb0, tb1):
+            res = sb("res%d_%d" % (nb, tb0), [P, (tb1 - tb0) * P], F32)
+            nc.scalar.copy(res[:], back[:, 0 : (tb1 - tb0) * P])
+            nc.scalar.dma_start(out[nb * P : (nb + 1) * P, tb0 * P : tb1 * P], res[:])
 
-        def store_sum(nb, back):
-            for (t0, t1), part in zip(pieces, back):
-                res = sb("res%d_%d" % (nb, t0), [P, t1 - t0], F32)
-                nc.scalar.copy(res[:], part[:, 0 : t1 - t0])
-                nc.sync.dma_start(out[nb * P : (nb + 1) * P, t0:t1], res[:])
+        def open_sums(nb, short):
+            sums = [bank(tb, "sum%d_%d" % (nb, tb)) for tb in range(TB)]
+            for r in (3, 2, 1):
+                add_term(sums, nb, r, 0, TB, r == 3, lambda tb: r == 1 and tb in short)
+            return sums
 
-        store_sum(0, summed(0, (3, 2, 1, 0), (5, 6)))
-        partial = summed(2, (3, 2, 1), (7, 6))
-        store_sum(1, summed(1, (3, 2, 1, 0), (5, 0)))
-        last = [weighted(2, 0, t0, t1) for t0, t1 in pieces]
-        for (t0, t1), prod, part in zip(pieces, last, partial):
+        def finish(sums, nb, pieces):
+            for tb0, tb1, b in pieces:
+                add_term(sums, nb, 0, tb0, tb1, False, lambda tb: True)
+                store(turn_back(sums, nb, tb0, tb1, b), nb, tb0, tb1)
+
+        sums = open_sums(0, ())
+        add_term(sums, 0, 0, 0, TB, False, lambda tb: True)
+        for tb0, tb1, b in ((0, 4, 5), (4, 5, 6)):
+            store(turn_back(sums, 0, tb0, tb1, b), 0, tb0, tb1)
+        sums = open_sums(2, range(1, TB))
+        finish(sums, 2, ((0, 1, 6),))
+        partial = turn_back(sums, 2, 1, TB, 7)
+        finish(open_sums(1, ()), 1, ((0, 2, 5), (2, 4, 6), (4, 5, 0)))
+
+        def add_last(prod, t0, t1):
             res = sb("res2_%d" % t0, [P, t1 - t0], F32)
-            nc.vector.tensor_tensor(res[:], part[:, 0 : t1 - t0], prod[:], ADD)
+            nc.vector.tensor_tensor(res[:], partial[:, t0 - P : t1 - P], prod[:], ADD)
             nc.sync.dma_start(out[2 * P : 3 * P, t0:t1], res[:])
+
+        pieces = ((P, 3 * P), (3 * P, 4 * P), (4 * P, T))
+        waiting = None
+        for t0, t1 in pieces:
+            prod = weighted(2, 0, t0, t1)
+            if waiting is not None:
+                add_last(*waiting)
+            waiting = (prod, t0, t1)
+        add_last(*waiting)

@@ -207,10 +207,10 @@ def tile_moe_ecr_glu_gelu_kernel(tc, x_words, x_scales, w1_words, w1_scales, w3_
         results(0, 2, 4, 4)
         results(0, 4, 5, 2, nc.vector.tensor_copy)
         results(0, 5, 6, 6)
-        results(2, 0, 4, 5)
-        results(2, 4, 6, 6)
-        results(1, 0, 4, 7)
+        results(1, 0, 4, 5)
         results(1, 4, 6, 6)
+        results(2, 0, 4, 7)
+        results(2, 4, 6, 6)
 
         def weighted(nb, r, t0, t1):
             prod = sb("prod%d_%d_%d" % (nb, r, t0), [P, t1 - t0], F32)
@@ -222,7 +222,7 @@ def tile_moe_ecr_glu_gelu_kernel(tc, x_words, x_scales, w1_words, w1_scales, w3_
             for tb in range(tb0, tb1):
                 nc.tensor.matmul(
                     sums[tb][:, 0:P], prod[:, (tb - tb0) * P : (tb - tb0 + 1) * P], ident[:],
-                    start=first, stop=last(tb), is_transpose=True,
+                    start=first, stop=last, is_transpose=True,
                 )
 
         def turn_back(sums, nb, tb0, tb1, b):
@@ -241,36 +241,30 @@ def tile_moe_ecr_glu_gelu_kernel(tc, x_words, x_scales, w1_words, w1_scales, w3_
             nc.scalar.copy(res[:], back[:, 0 : (tb1 - tb0) * P])
             nc.scalar.dma_start(out[nb * P : (nb + 1) * P, tb0 * P : tb1 * P], res[:])
 
-        def open_sums(nb, short):
+        def open_sums(nb):
             sums = [bank(tb, "sum%d_%d" % (nb, tb)) for tb in range(TB)]
-            for r in (3, 2, 1):
-                add_term(sums, nb, r, 0, TB, r == 3, lambda tb: r == 1 and tb in short)
+            for r in (3, 2, 1, 0):
+                add_term(sums, nb, r, 0, TB, r == 3, r == 0)
             return sums
 
-        def finish(sums, nb, pieces):
-            for tb0, tb1, b in pieces:
-                add_term(sums, nb, 0, tb0, tb1, False, lambda tb: True)
+        for nb in range(NB - 1):
+            sums = open_sums(nb)
+            for tb0, tb1, b in ((0, 4, 5), (4, 5, 6)):
                 store(turn_back(sums, nb, tb0, tb1, b), nb, tb0, tb1)
 
-        sums = open_sums(0, ())
-        add_term(sums, 0, 0, 0, TB, False, lambda tb: True)
-        for tb0, tb1, b in ((0, 4, 5), (4, 5, 6)):
-            store(turn_back(sums, 0, tb0, tb1, b), 0, tb0, tb1)
-        sums = open_sums(2, range(1, TB))
-        finish(sums, 2, ((0, 1, 6),))
-        partial = turn_back(sums, 2, 1, TB, 7)
-        finish(open_sums(1, ()), 1, ((0, 2, 5), (2, 4, 6), (4, 5, 0)))
+        def added(name, a, b):
+            res = sb(name, list(a.shape), F32)
+            nc.vector.tensor_tensor(res[:], a, b, ADD)
+            return res
 
-        def add_last(prod, t0, t1):
-            res = sb("res2_%d" % t0, [P, t1 - t0], F32)
-            nc.vector.tensor_tensor(res[:], partial[:, t0 - P : t1 - P], prod[:], ADD)
-            nc.sync.dma_start(out[2 * P : 3 * P, t0:t1], res[:])
-
-        pieces = ((P, 3 * P), (3 * P, 4 * P), (4 * P, T))
-        waiting = None
-        for t0, t1 in pieces:
-            prod = weighted(2, 0, t0, t1)
-            if waiting is not None:
-                add_last(*waiting)
-            waiting = (prod, t0, t1)
-        add_last(*waiting)
+        nb = NB - 1
+        terms = [weighted(nb, r, 0, T) for r in (3, 2, 1)]
+        partial = added("pair", terms[0][:], terms[1][:])
+        pieces = ((0, 3 * P), (3 * P, 4 * P), (4 * P, T))
+        last = [weighted(nb, 0, *pieces[0])]
+        partial = added("triple", partial[:], terms[2][:])
+        for i, (t0, t1) in enumerate(pieces):
+            if i + 1 < len(pieces):
+                last.append(weighted(nb, 0, *pieces[i + 1]))
+            res = added("res%d_%d" % (nb, t0), partial[:, t0:t1], last[i][:])
+            nc.sync.dma_start(out[nb * P : (nb + 1) * P, t0:t1], res[:])

@@ -48,17 +48,17 @@ def tile_moe_ecr_glu_gelu_kernel(tc, x_words, x_scales, w1_words, w1_scales, w3_
             engine.memset(plane[:].bitcast(I32), 0)
             return plane
 
-        xs = zero_plane(nc.gpsimd, "xs", T)
+        xs = zero_plane(nc.vector, "xs", T)
         w1s = zero_plane(nc.vector, "w1s", E * H)
         w3s = zero_plane(nc.vector, "w3s", E * H)
         w2s = zero_plane(nc.vector, "w2s", E * N)
         ident = sb("ident", [P, P], F32)
         make_identity(nc, ident[:])
 
-        def load_row(queue, plane, scales, r):
+        def load_row(plane, scales, r):
             src = scales.rearrange("e (q r) c -> r q e c", r=4)[r]
             dst = plane[r:P:32, :].bitcast(I32).rearrange("q (e c) -> q e c", e=scales.shape[0])
-            queue.dma_start(dst, src.bitcast(I32))
+            nc.sync.dma_start(dst, src.bitcast(I32))
 
         def load_words(name, words, e0, e1, c0, c1):
             t = sb(name, [P, e1 - e0, c1 - c0], U8)
@@ -74,25 +74,25 @@ def tile_moe_ecr_glu_gelu_kernel(tc, x_words, x_scales, w1_words, w1_scales, w3_
         xw = sb("xw", [P, T], I32)
         nc.sync.dma_start(xw[:], x_words[0].rearrange("p t r -> p (t r)").bitcast(I32))
         for r in range(4):
-            load_row(nc.sync, xs, x_scales, r)
+            load_row(xs, x_scales, r)
         offs_sb = load_list("offs_sb", offs)
         w1w = [load_words("w1w0", w1_words, 0, PAIR, 0, 2 * H)]
         w3w = [load_words("w3w0", w3_words, 0, PAIR, 0, 2 * H)]
         for r in range(4):
-            load_row(nc.sync if r < 3 else nc.gpsimd, w1s, w1_rows, r)
+            load_row(w1s, w1_rows, r)
         for r in range(4):
-            load_row(nc.sync if r < 3 else nc.gpsimd, w3s, w3_rows, r)
-        for r in range(2):
-            load_row(nc.gpsimd, w2s, w2_rows, r)
+            load_row(w3s, w3_rows, r)
         for g in range(1, E // PAIR):
             w1w.append(load_words("w1w%d" % g, w1_words, PAIR * g, PAIR * (g + 1), 0, 2 * H))
             w3w.append(load_words("w3w%d" % g, w3_words, PAIR * g, PAIR * (g + 1), 0, 2 * H))
+        pos = {0: load_list("pos_sb0", pos1)}
         w2_first = load_words("w2_first", w2_words, 0, E, 0, 2 * P)
-        for r in range(2, 4):
-            load_row(nc.sync, w2s, w2_rows, r)
-        pos = [load_list("pos_sb%d" % r, lst) for r, lst in enumerate((pos1, pos2, pos3, pos4))]
+        for r in range(4):
+            load_row(w2s, w2_rows, r)
         gates_rest = sb("gates_rest", [P, TOP - 1, T], F32)
         nc.sync.dma_start(gates_rest[:], gate[1:TOP, 0:P, :].rearrange("r p t -> p r t"))
+        for r, lst in ((3, pos4), (2, pos3), (1, pos2)):
+            pos[r] = load_list("pos_sb%d" % r, lst)
         w2_rest = load_words("w2_rest", w2_words, 0, E, 2 * P, 2 * N)
         gate_first = sb("gate_first", [P, T], F32)
         nc.sync.dma_start(gate_first[:], gate[0, 0:P, :])
@@ -101,7 +101,7 @@ def tile_moe_ecr_glu_gelu_kernel(tc, x_words, x_scales, w1_words, w1_scales, w3_
         y = []
         for nb in range(NB):
             t = sb("y%d" % nb, [P, S + PAD], F32)
-            nc.vector.memset(t[:, S:], 0.0)
+            nc.gpsimd.memset(t[:, S:], 0.0)
             y.append(t)
 
         xg, xsg = {}, {}

@@ -12,6 +12,7 @@ TB = T // P
 BANK = 512
 WARM_PASSES = 8
 PAIR = 2
+TURNED = 2
 A_BANKS = (0, 2, 4, 6, 0, 4)
 B_BANKS = (1, 3, 5, 7, 2, 6)
 
@@ -207,64 +208,58 @@ def tile_moe_ecr_glu_gelu_kernel(tc, x_words, x_scales, w1_words, w1_scales, w3_
         results(0, 2, 4, 4)
         results(0, 4, 5, 2, nc.vector.tensor_copy)
         results(0, 5, 6, 6)
-        results(1, 0, 4, 5)
-        results(1, 4, 6, 6)
-        results(2, 0, 4, 7)
-        results(2, 4, 6, 6)
+        results(2, 0, 4, 3)
+        results(2, 4, 6, 5)
+        results(1, 0, 4, 7)
+        results(1, 4, 6, 4)
 
         def weighted(nb, r, t0, t1):
             prod = sb("prod%d_%d_%d" % (nb, r, t0), [P, t1 - t0], F32)
             nc.vector.tensor_tensor(prod[:], y[nb][:].indirect(pos[r][:, t0 // 16 : t1 // 16]), gates[r][:, t0:t1], MULT)
             return prod
 
-        def add_term(sums, nb, r, tb0, tb1, first, last):
-            prod = weighted(nb, r, tb0 * P, tb1 * P)
-            for tb in range(tb0, tb1):
-                nc.tensor.matmul(
-                    sums[tb][:, 0:P], prod[:, (tb - tb0) * P : (tb - tb0 + 1) * P], ident[:],
-                    start=first, stop=last, is_transpose=True,
-                )
-
-        def turn_back(sums, nb, tb0, tb1, b):
-            by_token = []
-            for tb in range(tb0, tb1):
-                z = sb("z%d_%d" % (nb, tb), [P, P], F32)
-                nc.scalar.copy(z[:], sums[tb][:, 0:P])
-                by_token.append(z)
-            back = bank(b, "back%d_%d" % (nb, tb0))
-            for i, z in enumerate(by_token):
-                nc.tensor.transpose(back[:, i * P : (i + 1) * P], z[:], ident[:])
-            return back
-
-        def store(back, nb, tb0, tb1):
-            res = sb("res%d_%d" % (nb, tb0), [P, (tb1 - tb0) * P], F32)
-            nc.scalar.copy(res[:], back[:, 0 : (tb1 - tb0) * P])
-            nc.scalar.dma_start(out[nb * P : (nb + 1) * P, tb0 * P : tb1 * P], res[:])
-
-        def open_sums(nb):
-            sums = [bank(tb, "sum%d_%d" % (nb, tb)) for tb in range(TB)]
+        def summed(nb, tb0, tb1, banks):
+            groups = [(g0, min(g0 + 4, tb1)) for g0 in range(tb0, tb1, 4)]
+            sums = [bank(b, "sum%d_%d" % (nb, g0)) for (g0, g1), b in zip(groups, banks)]
             for r in (3, 2, 1, 0):
-                add_term(sums, nb, r, 0, TB, r == 3, r == 0)
-            return sums
+                prod = weighted(nb, r, tb0 * P, tb1 * P)
+                for (g0, g1), acc in zip(groups, sums):
+                    for tb in range(g0, g1):
+                        nc.tensor.matmul(
+                            acc[:, (tb - g0) * P : (tb - g0 + 1) * P], prod[:, (tb - tb0) * P : (tb - tb0 + 1) * P], ident[:],
+                            start=(r == 3 and tb == g0), stop=(r == 0 and tb == g1 - 1), is_transpose=True,
+                        )
+            return list(zip(groups, sums))
 
-        for nb in range(NB - 1):
-            sums = open_sums(nb)
-            for tb0, tb1, b in ((0, 4, 5), (4, 5, 6)):
-                store(turn_back(sums, nb, tb0, tb1, b), nb, tb0, tb1)
+        def store(nb, sums, banks):
+            for ((g0, g1), acc), b in zip(sums, banks):
+                width = (g1 - g0) * P
+                by_token = sb("z%d_%d" % (nb, g0), [P, width], F32)
+                nc.scalar.copy(by_token[:], acc[:, 0:width])
+                back = bank(b, "back%d_%d" % (nb, g0))
+                for at in range(0, width, P):
+                    nc.tensor.transpose(back[:, at : at + P], by_token[:, at : at + P], ident[:])
+                res = sb("res%d_%d" % (nb, g0), [P, width], F32)
+                nc.scalar.copy(res[:], back[:, 0:width])
+                nc.scalar.dma_start(out[nb * P : (nb + 1) * P, g0 * P : g1 * P], res[:])
+
+        store(0, summed(0, 0, TB, (0, 1)), (5, 6))
+        store(2, summed(2, 0, TURNED, (2,)), (7,))
+        store(1, summed(1, 0, TB, (3, 4)), (0, 1))
 
         def added(name, a, b):
             res = sb(name, list(a.shape), F32)
             nc.vector.tensor_tensor(res[:], a, b, ADD)
             return res
 
-        nb = NB - 1
-        terms = [weighted(nb, r, 0, T) for r in (3, 2, 1)]
+        nb, first = NB - 1, TURNED * P
+        terms = [weighted(nb, r, first, T) for r in (3, 2, 1)]
         partial = added("pair", terms[0][:], terms[1][:])
-        pieces = ((0, 3 * P), (3 * P, 4 * P), (4 * P, T))
+        pieces = ((first, T - P), (T - P, T))
         last = [weighted(nb, 0, *pieces[0])]
         partial = added("triple", partial[:], terms[2][:])
         for i, (t0, t1) in enumerate(pieces):
             if i + 1 < len(pieces):
                 last.append(weighted(nb, 0, *pieces[i + 1]))
-            res = added("res%d_%d" % (nb, t0), partial[:, t0:t1], last[i][:])
+            res = added("res%d_%d" % (nb, t0), partial[:, t0 - first : t1 - first], last[i][:])
             nc.sync.dma_start(out[nb * P : (nb + 1) * P, t0:t1], res[:])

@@ -86,18 +86,18 @@ def tile_moe_ecr_glu_gelu_kernel(tc, x_words, x_scales, w1_words, w1_scales, w3_
         for g in range(1, E // PAIR):
             w1w.append(load_words("w1w%d" % g, w1_words, PAIR * g, PAIR * (g + 1), 0, 2 * H))
             w3w.append(load_words("w3w%d" % g, w3_words, PAIR * g, PAIR * (g + 1), 0, 2 * H))
-        pos = {0: load_list("pos_sb0", pos1)}
-        w2_first = load_words("w2_first", w2_words, 0, E, 0, 2 * P)
+        pos = {r: load_list("pos_sb%d" % r, lst) for r, lst in ((3, pos4), (2, pos3))}
+        w2w = load_words("w2w", w2_words, 0, E, 0, 2 * N)
+        for r, lst in ((1, pos2), (0, pos1)):
+            pos[r] = load_list("pos_sb%d" % r, lst)
         for r in range(4):
             load_row(w2s, w2_rows, r)
-        gates_rest = sb("gates_rest", [P, TOP - 1, T], F32)
-        nc.sync.dma_start(gates_rest[:], gate[1:TOP, 0:P, :].rearrange("r p t -> p r t"))
-        for r, lst in ((3, pos4), (2, pos3), (1, pos2)):
-            pos[r] = load_list("pos_sb%d" % r, lst)
-        w2_rest = load_words("w2_rest", w2_words, 0, E, 2 * P, 2 * N)
-        gate_first = sb("gate_first", [P, T], F32)
-        nc.sync.dma_start(gate_first[:], gate[0, 0:P, :])
-        gates = [gate_first[:]] + [gates_rest[:, r, :] for r in range(TOP - 1)]
+        gates = {}
+        for r0, r1 in ((2, 4), (1, 2), (0, 1)):
+            t = sb("gates%d" % r0, [P, r1 - r0, T], F32)
+            nc.sync.dma_start(t[:], gate[r0:r1, 0:P, :].rearrange("r p t -> p r t"))
+            for r in range(r0, r1):
+                gates[r] = t[:, r - r0, :]
 
         y = []
         for nb in range(NB):
@@ -177,7 +177,7 @@ def tile_moe_ecr_glu_gelu_kernel(tc, x_words, x_scales, w1_words, w1_scales, w3_
         def second_layer(dst, e, nb):
             nc.tensor.matmul_mx(
                 dst,
-                lhsT=(w2_first[:, e, :] if nb == 0 else w2_rest[:, e, 2 * P * (nb - 1) : 2 * P * nb]).bitcast(FP4X4),
+                lhsT=w2w[:, e, 2 * P * nb : 2 * P * (nb + 1)].bitcast(FP4X4),
                 lhsT_scale=w2s[:, e * N + P * nb : e * N + P * (nb + 1)],
                 rhs=hq[e].bitcast(FP8X4),
                 rhs_scale=hs[e],
@@ -208,10 +208,10 @@ def tile_moe_ecr_glu_gelu_kernel(tc, x_words, x_scales, w1_words, w1_scales, w3_
         results(0, 2, 4, 4)
         results(0, 4, 5, 2, nc.vector.tensor_copy)
         results(0, 5, 6, 6)
-        results(2, 0, 4, 3)
-        results(2, 4, 6, 5)
-        results(1, 0, 4, 7)
-        results(1, 4, 6, 4)
+        results(1, 0, 4, 3)
+        results(1, 4, 6, 5)
+        results(2, 0, 4, 7)
+        results(2, 4, 6, 4)
 
         def weighted(nb, r, t0, t1):
             prod = sb("prod%d_%d_%d" % (nb, r, t0), [P, t1 - t0], F32)
@@ -244,8 +244,8 @@ def tile_moe_ecr_glu_gelu_kernel(tc, x_words, x_scales, w1_words, w1_scales, w3_
                 nc.scalar.dma_start(out[nb * P : (nb + 1) * P, g0 * P : g1 * P], res[:])
 
         store(0, summed(0, 0, TB, (0, 1)), (5, 6))
-        store(2, summed(2, 0, TURNED, (2,)), (7,))
-        store(1, summed(1, 0, TB, (3, 4)), (0, 1))
+        store(1, summed(1, 0, TB, (2, 3)), (7, 4))
+        store(2, summed(2, 0, TURNED, (0,)), (1,))
 
         def added(name, a, b):
             res = sb(name, list(a.shape), F32)

@@ -147,20 +147,20 @@ def tile_moe_ecr_glu_gelu_kernel(tc, x_words, x_scales, w1_words, w1_scales, w3_
                     stop=True,
                 )
             tag = "shared" if e == E - 1 else "act%d" % e
-            act[e] = keep.tile([P, 2, P, 2], F32, name="act%d" % e, tag=tag, align_bytes=64)
-            nc.scalar.activation(act[e][:], a_ps[e][:].rearrange("s (p u d) -> s u p d", u=2, d=2), GELU)
+            act[e] = keep.tile([P, H], F32, name="act%d" % e, tag=tag, align_bytes=64)
+            nc.scalar.activation(act[e][:], a_ps[e][:], GELU)
 
         def product(e):
-            hh[e] = keep.tile([P, 2, P, 2], BF16, name="h%d" % e, tag="h%d" % e, align_bytes=64)
-            nc.vector.tensor_tensor(hh[e][:], b_ps[e][:].rearrange("s (p u d) -> s u p d", u=2, d=2), act[e][:], MULT)
+            hh[e] = keep.tile([P, H], BF16, name="h%d" % e, tag="h%d" % e, align_bytes=64)
+            nc.vector.tensor_tensor(hh[e][:], b_ps[e][:], act[e][:], MULT)
 
         def turn(e0, e1, b, move=nc.scalar.copy):
             turned = bank(b, "turned%d" % e0)
             for e in range(e0, e1):
-                pairs = hh[e][:].rearrange("s u p d -> s (u p d)").bitcast(F32)
+                pairs = hh[e][:].bitcast(F32)
                 for u in range(2):
                     at = (2 * (e - e0) + u) * P
-                    nc.tensor.transpose(turned[:, at : at + P], pairs[:, u * P : (u + 1) * P], ident[:])
+                    nc.tensor.transpose(turned[:, at : at + P], pairs[:, u : 2 * P : 2], ident[:])
             move(
                 ht[:, e0 * 4 * C : e1 * 4 * C].bitcast(F32).rearrange("p (e s u) -> p e s u", e=e1 - e0, u=2),
                 turned[:, 0 : 2 * P * (e1 - e0)].rearrange("p (e u s) -> p e s u", e=e1 - e0, u=2),

@@ -10,9 +10,10 @@ P = 128
 NB = N // P
 TB = T // P
 BANK = 512
-WARM_PASSES = 8
+WARM_PASSES = 6
 PAIR = 2
 TURNED = 2
+FULLEST = 0
 A_BANKS = (0, 2, 4, 6, 0, 4)
 B_BANKS = (1, 3, 5, 7, 2, 6)
 
@@ -26,6 +27,7 @@ FP8X4 = mybir.dt.float8_e4m3fn_x4
 FP4X4 = mybir.dt.float4_e2m1fn_x4
 MULT = mybir.AluOpType.mult
 ADD = mybir.AluOpType.add
+COPY = mybir.ActivationFunctionType.Copy
 GELU = mybir.ActivationFunctionType.Gelu_apprx_tanh
 
 FLOPS = 2 * S * (2 * K * H + H * N)
@@ -208,14 +210,24 @@ def tile_moe_ecr_glu_gelu_kernel(tc, x_words, x_scales, w1_words, w1_scales, w3_
         results(0, 2, 4, 4)
         results(0, 4, 5, 2, nc.vector.tensor_copy)
         results(0, 5, 6, 6)
+        picked = {}
+
+        def pick(nb):
+            picked[nb] = sb("picked%d" % nb, [P, T], F32)
+            nc.scalar.activation(picked[nb][:], y[nb][:].indirect(pos[FULLEST][:]), COPY)
+
         results(1, 0, 4, 3)
         results(1, 4, 6, 5)
+        pick(0)
         results(2, 0, 4, 7)
         results(2, 4, 6, 4)
+        pick(1)
+        pick(2)
 
         def weighted(nb, r, t0, t1):
             prod = sb("prod%d_%d_%d" % (nb, r, t0), [P, t1 - t0], F32)
-            nc.vector.tensor_tensor(prod[:], y[nb][:].indirect(pos[r][:, t0 // 16 : t1 // 16]), gates[r][:, t0:t1], MULT)
+            values = picked[nb][:, t0:t1] if r == FULLEST else y[nb][:].indirect(pos[r][:, t0 // 16 : t1 // 16])
+            nc.vector.tensor_tensor(prod[:], values, gates[r][:, t0:t1], MULT)
             return prod
 
         def summed(nb, tb0, tb1, banks):

@@ -10,7 +10,6 @@ P = 128
 NB = N // P
 TB = T // P
 BANK = 512
-WARM_PASSES = 6
 PAIR = 2
 TURNED = 2
 FULLEST = 0
@@ -121,18 +120,6 @@ def tile_moe_ecr_glu_gelu_kernel(tc, x_words, x_scales, w1_words, w1_scales, w3_
 
         a_ps, b_ps, act, hh, hq, hs = {}, {}, {}, {}, {}, {}
         ht = sb("ht", [P, E * 4 * C], BF16)
-
-        warm = bank(7, "warm")
-        for i in range(WARM_PASSES):
-            nc.tensor.matmul_mx(
-                warm[:, (i % 4) * P : (i % 4 + 1) * P],
-                lhsT=xg[0].bitcast(FP8X4),
-                lhsT_scale=xsg[0],
-                rhs=w1w[0][:, 0, 0 : 2 * P].bitcast(FP4X4),
-                rhs_scale=xsg[0],
-                start=True,
-                stop=True,
-            )
 
         def first_layer(e):
             g, j = divmod(e, PAIR)

@@ -75,9 +75,9 @@ def tile_moe_ecr_glu_gelu_kernel(tc, x_words, x_scales, w1_words, w1_scales, w3_
         w1_rows, w3_rows, w2_rows = (s.rearrange("e o q c -> (e o) q c") for s in (w1_scales, w3_scales, w2_scales))
         xw = sb("xw", [P, T], I32)
         nc.sync.dma_start(xw[:], x_words[0].rearrange("p t r -> p (t r)").bitcast(I32))
+        offs_sb = load_list("offs_sb", offs)
         for r in range(4):
             load_row(xs, x_scales, r)
-        offs_sb = load_list("offs_sb", offs)
         w1w = [load_words("w1w0", w1_words, 0, PAIR, 0, 2 * H)]
         w3w = [load_words("w3w0", w3_words, 0, PAIR, 0, 2 * H)]
         for r in range(4):
@@ -114,8 +114,9 @@ def tile_moe_ecr_glu_gelu_kernel(tc, x_words, x_scales, w1_words, w1_scales, w3_
             for e in range(e0, e1):
                 into[e] = t[:, (e - e0) * C : (e - e0 + 1) * C]
 
-        for e0, e1 in ((0, 1), (1, 3), (3, 6)):
+        for e0, e1 in ((0, 3), (3, 6)):
             gather(xg, "xg", xw[:].bitcast(U32), U32, e0, e1)
+        for e0, e1 in ((0, 1), (1, 3), (3, 6)):
             gather(xsg, "xsg", xs[:], U8, e0, e1)
 
         a_ps, b_ps, act, hh, hq, hs = {}, {}, {}, {}, {}, {}

@@ -218,8 +218,8 @@ def tile_moe_ecr_glu_gelu_kernel(tc, x_words, x_scales, w1_words, w1_scales, w3_
             nc.vector.tensor_tensor(prod[:], values, gates[r][:, t0:t1], MULT)
             return prod
 
-        def summed(nb, tb0, tb1, banks):
-            groups = [(g0, min(g0 + 4, tb1)) for g0 in range(tb0, tb1, 4)]
+        def summed(nb, groups, banks):
+            tb0, tb1 = groups[0][0], groups[-1][1]
             sums = [bank(b, "sum%d_%d" % (nb, g0)) for (g0, g1), b in zip(groups, banks)]
             for r in (3, 2, 1, 0):
                 prod = weighted(nb, r, tb0 * P, tb1 * P)
@@ -229,23 +229,26 @@ def tile_moe_ecr_glu_gelu_kernel(tc, x_words, x_scales, w1_words, w1_scales, w3_
                             acc[:, (tb - g0) * P : (tb - g0 + 1) * P], prod[:, (tb - tb0) * P : (tb - tb0 + 1) * P], ident[:],
                             start=(r == 3 and tb == g0), stop=(r == 0 and tb == g1 - 1), is_transpose=True,
                         )
-            return list(zip(groups, sums))
+            by_token = []
+            for (g0, g1), acc in zip(groups, sums):
+                t = sb("z%d_%d" % (nb, g0), [P, (g1 - g0) * P], F32)
+                nc.scalar.copy(t[:], acc[:, 0 : (g1 - g0) * P])
+                by_token.extend(t[:, at : at + P] for at in range(0, (g1 - g0) * P, P))
+            return by_token
 
-        def store(nb, sums, banks):
-            for ((g0, g1), acc), b in zip(sums, banks):
-                width = (g1 - g0) * P
-                by_token = sb("z%d_%d" % (nb, g0), [P, width], F32)
-                nc.scalar.copy(by_token[:], acc[:, 0:width])
+        def store(nb, by_token, banks, queue):
+            for g0, b in zip(range(0, len(by_token), 4), banks):
+                g1 = min(g0 + 4, len(by_token))
                 back = bank(b, "back%d_%d" % (nb, g0))
-                for at in range(0, width, P):
-                    nc.tensor.transpose(back[:, at : at + P], by_token[:, at : at + P], ident[:])
-                res = sb("res%d_%d" % (nb, g0), [P, width], F32)
-                nc.scalar.copy(res[:], back[:, 0:width])
-                nc.scalar.dma_start(out[nb * P : (nb + 1) * P, g0 * P : g1 * P], res[:])
+                for tb in range(g0, g1):
+                    nc.tensor.transpose(back[:, (tb - g0) * P : (tb - g0 + 1) * P], by_token[tb], ident[:])
+                res = sb("res%d_%d" % (nb, g0), [P, (g1 - g0) * P], F32)
+                nc.scalar.copy(res[:], back[:, 0 : (g1 - g0) * P])
+                queue.dma_start(out[nb * P : (nb + 1) * P, g0 * P : g1 * P], res[:])
 
-        store(0, summed(0, 0, TB, (0, 1)), (5, 6))
-        store(1, summed(1, 0, TB, (2, 3)), (7, 4))
-        store(2, summed(2, 0, TURNED, (0,)), (1,))
+        store(0, summed(0, ((0, 4), (4, 5)), (0, 1)), (5, 6), nc.sync)
+        store(1, summed(1, ((0, 4), (4, 5)), (2, 3)), (7, 4), nc.scalar)
+        store(2, summed(2, ((0, 1), (1, 2)), (0, 2)), (1,), nc.scalar)
 
         def added(name, a, b):
             res = sb(name, list(a.shape), F32)

@@ -236,19 +236,29 @@ def tile_moe_ecr_glu_gelu_kernel(tc, x_words, x_scales, w1_words, w1_scales, w3_
                 by_token.extend(t[:, at : at + P] for at in range(0, (g1 - g0) * P, P))
             return by_token
 
-        def store(nb, by_token, banks, queue):
-            for g0, b in zip(range(0, len(by_token), 4), banks):
-                g1 = min(g0 + 4, len(by_token))
-                back = bank(b, "back%d_%d" % (nb, g0))
-                for tb in range(g0, g1):
-                    nc.tensor.transpose(back[:, (tb - g0) * P : (tb - g0 + 1) * P], by_token[tb], ident[:])
-                res = sb("res%d_%d" % (nb, g0), [P, (g1 - g0) * P], F32)
-                nc.scalar.copy(res[:], back[:, 0 : (g1 - g0) * P])
-                queue.dma_start(out[nb * P : (nb + 1) * P, g0 * P : g1 * P], res[:])
+        def store(tiles, b, queue):
+            name = "%d_%d" % tiles[0][:2]
+            back = bank(b, "back" + name)
+            for i, (nb, tb, by_token) in enumerate(tiles):
+                nc.tensor.transpose(back[:, i * P : (i + 1) * P], by_token, ident[:])
+            res = sb("res" + name, [P, len(tiles) * P], F32)
+            nc.scalar.copy(res[:], back[:, 0 : len(tiles) * P])
+            for nb in sorted(set(tile[0] for tile in tiles)):
+                at = [i for i, tile in enumerate(tiles) if tile[0] == nb]
+                t0 = tiles[at[0]][1] * P
+                queue.dma_start(out[nb * P : (nb + 1) * P, t0 : t0 + len(at) * P], res[:, at[0] * P : (at[-1] + 1) * P])
 
-        store(0, summed(0, ((0, 4), (4, 5)), (0, 1)), (5, 6), nc.sync)
-        store(1, summed(1, ((0, 4), (4, 5)), (2, 3)), (7, 4), nc.scalar)
-        store(2, summed(2, ((0, 1), (1, 2)), (0, 2)), (1,), nc.scalar)
+        def tiles_of(nb, groups, banks):
+            return [(nb, tb, t) for tb, t in enumerate(summed(nb, groups, banks))]
+
+        block0 = tiles_of(0, ((0, 4), (4, 5)), (0, 1))
+        block1 = tiles_of(1, ((0, 4), (4, 5)), (2, 3))
+        store(block0[:4], 5, nc.sync)
+        store(block0[4:], 6, nc.sync)
+        store(block1[:4], 7, nc.scalar)
+        block2 = tiles_of(2, ((0, 1), (1, 2)), (2, 3))
+        store(block1[4:], 4, nc.scalar)
+        store(block2, 0, nc.scalar)
 
         def added(name, a, b):
             res = sb(name, list(a.shape), F32)

@@ -198,36 +198,43 @@ def tile_moe_ecr_glu_gelu_kernel(tc, x_words, x_scales, w1_words, w1_scales, w3_
         results(0, 2, 4, 4)
         results(0, 4, 5, 2, nc.vector.tensor_copy)
         results(0, 5, 6, 6)
+        first = TURNED * P
         picked = {}
 
-        def pick(nb):
-            picked[nb] = sb("picked%d" % nb, [P, T], F32)
-            nc.scalar.activation(picked[nb][:], y[nb][:].indirect(pos[FULLEST][:]), COPY)
+        def pick(nb, r, t0):
+            t = sb("picked%d_%d" % (nb, r), [P, T - t0], F32)
+            nc.scalar.activation(t[:], y[nb][:].indirect(pos[r][:, t0 // 16 :]), COPY)
+            picked[nb, r] = (t, t0)
 
         results(1, 0, 4, 3)
         results(1, 4, 6, 5)
-        pick(0)
+        pick(0, 0, 0)
         results(2, 0, 4, 7)
         results(2, 4, 6, 4)
-        pick(1)
-        pick(2)
+        pick(1, 0, 0)
+        pick(2, 0, 0)
+        pick(2, 1, first)
 
         def weighted(nb, r, t0, t1):
             prod = sb("prod%d_%d_%d" % (nb, r, t0), [P, t1 - t0], F32)
-            values = picked[nb][:, t0:t1] if r == FULLEST else y[nb][:].indirect(pos[r][:, t0 // 16 : t1 // 16])
+            t, at = picked.get((nb, r), (None, T))
+            values = t[:, t0 - at : t1 - at] if t0 >= at else y[nb][:].indirect(pos[r][:, t0 // 16 : t1 // 16])
             nc.vector.tensor_tensor(prod[:], values, gates[r][:, t0:t1], MULT)
             return prod
 
-        def summed(nb, groups, banks):
-            tb0, tb1 = groups[0][0], groups[-1][1]
+        def added(name, a, b):
+            res = sb(name, list(a.shape), F32)
+            nc.vector.tensor_tensor(res[:], a, b, ADD)
+            return res
+
+        def summed(nb, prods, groups, banks):
             sums = [bank(b, "sum%d_%d" % (nb, g0)) for (g0, g1), b in zip(groups, banks)]
-            for r in (3, 2, 1, 0):
-                prod = weighted(nb, r, tb0 * P, tb1 * P)
+            for i, prod in enumerate(prods):
                 for (g0, g1), acc in zip(groups, sums):
                     for tb in range(g0, g1):
                         nc.tensor.matmul(
-                            acc[:, (tb - g0) * P : (tb - g0 + 1) * P], prod[:, (tb - tb0) * P : (tb - tb0 + 1) * P], ident[:],
-                            start=(r == 3 and tb == g0), stop=(r == 0 and tb == g1 - 1), is_transpose=True,
+                            acc[:, (tb - g0) * P : (tb - g0 + 1) * P], prod[:, tb * P : (tb + 1) * P], ident[:],
+                            start=(i == 0 and tb == g0), stop=(i == TOP - 1 and tb == g1 - 1), is_transpose=True,
                         )
             by_token = []
             for (g0, g1), acc in zip(groups, sums):
@@ -236,43 +243,32 @@ def tile_moe_ecr_glu_gelu_kernel(tc, x_words, x_scales, w1_words, w1_scales, w3_
                 by_token.extend(t[:, at : at + P] for at in range(0, (g1 - g0) * P, P))
             return by_token
 
-        def store(tiles, b, queue):
-            name = "%d_%d" % tiles[0][:2]
-            back = bank(b, "back" + name)
-            for i, (nb, tb, by_token) in enumerate(tiles):
-                nc.tensor.transpose(back[:, i * P : (i + 1) * P], by_token, ident[:])
-            res = sb("res" + name, [P, len(tiles) * P], F32)
-            nc.scalar.copy(res[:], back[:, 0 : len(tiles) * P])
-            for nb in sorted(set(tile[0] for tile in tiles)):
-                at = [i for i, tile in enumerate(tiles) if tile[0] == nb]
-                t0 = tiles[at[0]][1] * P
-                queue.dma_start(out[nb * P : (nb + 1) * P, t0 : t0 + len(at) * P], res[:, at[0] * P : (at[-1] + 1) * P])
+        def store(nb, tb0, by_token, b, queue):
+            width = len(by_token) * P
+            back = bank(b, "back%d_%d" % (nb, tb0))
+            for i, t in enumerate(by_token):
+                nc.tensor.transpose(back[:, i * P : (i + 1) * P], t, ident[:])
+            res = sb("res%d_%d" % (nb, tb0), [P, width], F32)
+            nc.scalar.copy(res[:], back[:, 0:width])
+            queue.dma_start(out[nb * P : (nb + 1) * P, tb0 * P : tb0 * P + width], res[:])
 
-        def tiles_of(nb, groups, banks):
-            return [(nb, tb, t) for tb, t in enumerate(summed(nb, groups, banks))]
+        block0 = summed(0, [weighted(0, r, 0, T) for r in (3, 2, 1, 0)], ((0, 4), (4, 5)), (0, 1))
+        block1 = summed(1, [weighted(1, r, 0, T) for r in (3, 2, 1, 0)], ((0, 4), (4, 5)), (2, 3))
+        store(0, 0, block0[:4], 5, nc.sync)
+        store(0, 4, block0[4:], 6, nc.sync)
+        store(1, 0, block1[:4], 7, nc.sync)
 
-        block0 = tiles_of(0, ((0, 4), (4, 5)), (0, 1))
-        block1 = tiles_of(1, ((0, 4), (4, 5)), (2, 3))
-        store(block0[:4], 5, nc.sync)
-        store(block0[4:], 6, nc.sync)
-        store(block1[:4], 7, nc.scalar)
-        block2 = tiles_of(2, ((0, 1), (1, 2)), (2, 3))
-        store(block1[4:], 4, nc.scalar)
-        store(block2, 0, nc.scalar)
-
-        def added(name, a, b):
-            res = sb(name, list(a.shape), F32)
-            nc.vector.tensor_tensor(res[:], a, b, ADD)
-            return res
-
-        nb, first = NB - 1, TURNED * P
-        terms = [weighted(nb, r, first, T) for r in (3, 2, 1)]
-        partial = added("pair", terms[0][:], terms[1][:])
+        nb = NB - 1
+        whole = [weighted(nb, r, 0, T) for r in (0, 3)]
+        block2 = summed(nb, whole + [weighted(nb, r, 0, first) for r in (1, 2)], ((0, 1), (1, 2)), (2, 3))
+        store(1, 4, block1[4:], 4, nc.sync)
+        store(nb, 0, block2, 0, nc.scalar)
+        partial = added("pair", whole[0][:, first:], whole[1][:, first:])
+        third = weighted(nb, 2, first, T)
         pieces = ((first, T - P), (T - P, T))
-        last = [weighted(nb, 0, *pieces[0])]
-        partial = added("triple", partial[:], terms[2][:])
-        for i, (t0, t1) in enumerate(pieces):
-            if i + 1 < len(pieces):
-                last.append(weighted(nb, 0, *pieces[i + 1]))
-            res = added("res%d_%d" % (nb, t0), partial[:, t0 - first : t1 - first], last[i][:])
+        last = [weighted(nb, 1, *pieces[0])]
+        partial = added("triple", partial[:], third[:])
+        last.append(weighted(nb, 1, *pieces[1]))
+        for (t0, t1), term in zip(pieces, last):
+            res = added("end%d" % t0, partial[:, t0 - first : t1 - first], term[:])
             nc.sync.dma_start(out[nb * P : (nb + 1) * P, t0:t1], res[:])

@@ -122,20 +122,25 @@ def tile_moe_ecr_glu_gelu_kernel(tc, x_words, x_scales, w1_words, w1_scales, w3_
         a_ps, b_ps, act, hh, hq, hs = {}, {}, {}, {}, {}, {}
         ht = sb("ht", [P, E * 4 * C], BF16)
 
-        def first_layer(e):
+        def first_pass(dst, words, plane, e):
             g, j = divmod(e, PAIR)
-            a_ps[e] = bank(A_BANKS[e], "a%d" % e)
+            nc.tensor.matmul_mx(
+                dst[:],
+                lhsT=xg[e].bitcast(FP8X4),
+                lhsT_scale=xsg[e],
+                rhs=words[g][:, j, :].bitcast(FP4X4),
+                rhs_scale=plane[:, e * H : (e + 1) * H],
+                start=True,
+                stop=True,
+            )
+
+        def linear_side(e):
             b_ps[e] = bank(B_BANKS[e], "b%d" % e)
-            for dst, words, plane in ((a_ps[e], w1w[g][:, j, :], w1s), (b_ps[e], w3w[g][:, j, :], w3s)):
-                nc.tensor.matmul_mx(
-                    dst[:],
-                    lhsT=xg[e].bitcast(FP8X4),
-                    lhsT_scale=xsg[e],
-                    rhs=words.bitcast(FP4X4),
-                    rhs_scale=plane[:, e * H : (e + 1) * H],
-                    start=True,
-                    stop=True,
-                )
+            first_pass(b_ps[e], w3w, w3s, e)
+
+        def gated_side(e):
+            a_ps[e] = bank(A_BANKS[e], "a%d" % e)
+            first_pass(a_ps[e], w1w, w1s, e)
             tag = "shared" if e == E - 1 else "act%d" % e
             act[e] = keep.tile([P, H], F32, name="act%d" % e, tag=tag, align_bytes=64)
             nc.scalar.activation(act[e][:], a_ps[e][:], GELU)
@@ -175,12 +180,15 @@ def tile_moe_ecr_glu_gelu_kernel(tc, x_words, x_scales, w1_words, w1_scales, w3_
                 stop=True,
             )
 
-        for e in range(E):
-            first_layer(e)
+        for e0 in range(0, E, PAIR):
+            for side in (gated_side, linear_side):
+                for e in range(e0, e0 + PAIR):
+                    side(e)
         for e in range(E):
             product(e)
         turn(0, 2, A_BANKS[4])
-        turn(2, 4, B_BANKS[0])
+        turn(2, 3, A_BANKS[5])
+        turn(3, 4, B_BANKS[4], nc.vector.tensor_copy)
         turn(4, 5, B_BANKS[1])
         turn(5, 6, B_BANKS[2])
         quantise(0, 2, "shared")

@@ -202,7 +202,7 @@ def tile_moe_ecr_glu_gelu_kernel(tc, x_words, x_scales, w1_words, w1_scales, w3_
                 second_layer(y_ps[:, (e - e0) * C : (e - e0 + 1) * C], e, nb)
             move(y[nb][:, e0 * C : e1 * C], y_ps[:, 0 : (e1 - e0) * C])
 
-        results(0, 0, 2, 7, nc.vector.tensor_copy)
+        results(0, 0, 2, 7)
         results(0, 2, 4, 4)
         results(0, 4, 5, 2, nc.vector.tensor_copy)
         results(0, 5, 6, 6)
@@ -221,7 +221,6 @@ def tile_moe_ecr_glu_gelu_kernel(tc, x_words, x_scales, w1_words, w1_scales, w3_
         results(2, 4, 6, 4)
         pick(1, 0, 0)
         pick(2, 0, 0)
-        pick(2, 1, first)
 
         def weighted(nb, r, t0, t1):
             prod = sb("prod%d_%d_%d" % (nb, r, t0), [P, t1 - t0], F32)

@@ -45,22 +45,28 @@ def tile_moe_ecr_glu_gelu_kernel(tc, x_words, x_scales, w1_words, w1_scales, w3_
         def bank(b, name):
             return psum.tile([P, BANK], F32, name=name, tag="bank%d" % b)
 
-        def zero_plane(engine, name, width):
+        def zero_plane(name, width):
             plane = sb(name, [P, width], U8)
-            engine.memset(plane[:].bitcast(I32), 0)
+            nc.vector.memset(plane[:].bitcast(I32), 0)
             return plane
 
-        xs = zero_plane(nc.vector, "xs", T)
-        w1s = zero_plane(nc.vector, "w1s", E * H)
-        w3s = zero_plane(nc.vector, "w3s", E * H)
-        w2s = zero_plane(nc.vector, "w2s", E * N)
+        xs = zero_plane("xs", T)
+        w3s = zero_plane("w3s", E * H)
+        w1s = zero_plane("w1s", E * H + 4)
+        w2s = zero_plane("w2s", E * N + 4)
         ident = sb("ident", [P, P], F32)
-        make_identity(nc, ident[:])
+        nc.vector.memset(ident[:], 0.0)
+        y = []
+        for nb in range(NB):
+            t = sb("y%d" % nb, [P, S + PAD], F32)
+            nc.vector.memset(t[:, S:], 0.0)
+            y.append(t)
 
-        def load_row(plane, scales, r):
+        def load_row(plane, scales, r, queue=nc.sync):
             src = scales.rearrange("e (q r) c -> r q e c", r=4)[r]
-            dst = plane[r:P:32, :].bitcast(I32).rearrange("q (e c) -> q e c", e=scales.shape[0])
-            nc.sync.dma_start(dst, src.bitcast(I32))
+            width = scales.shape[0] * scales.shape[2]
+            dst = plane[r:P:32, 0:width].bitcast(I32).rearrange("q (e c) -> q e c", e=scales.shape[0])
+            queue.dma_start(dst, src.bitcast(I32))
 
         def load_words(name, words, e0, e1, c0, c1):
             t = sb(name, [P, e1 - e0, c1 - c0], U8)
@@ -78,11 +84,14 @@ def tile_moe_ecr_glu_gelu_kernel(tc, x_words, x_scales, w1_words, w1_scales, w3_
         offs_sb = load_list("offs_sb", offs)
         for r in range(4):
             load_row(xs, x_scales, r)
-        w1w = [load_words("w1w0", w1_words, 0, PAIR, 0, 2 * H)]
-        w3w = [load_words("w3w0", w3_words, 0, PAIR, 0, 2 * H)]
         for r in range(4):
             load_row(w1s, w1_rows, r)
-        for r in range(4):
+        for r in (2, 3):
+            load_row(w3s, w3_rows, r, nc.gpsimd)
+        make_identity(nc, ident[:], nomemset=True)
+        w1w = [load_words("w1w0", w1_words, 0, PAIR, 0, 2 * H)]
+        w3w = [load_words("w3w0", w3_words, 0, PAIR, 0, 2 * H)]
+        for r in (0, 1):
             load_row(w3s, w3_rows, r)
         for g in range(1, E // PAIR):
             w1w.append(load_words("w1w%d" % g, w1_words, PAIR * g, PAIR * (g + 1), 0, 2 * H))
@@ -99,12 +108,6 @@ def tile_moe_ecr_glu_gelu_kernel(tc, x_words, x_scales, w1_words, w1_scales, w3_
             nc.sync.dma_start(t[:], gate[r0:r1, 0:P, :].rearrange("r p t -> p r t"))
             for r in range(r0, r1):
                 gates[r] = t[:, r - r0, :]
-
-        y = []
-        for nb in range(NB):
-            t = sb("y%d" % nb, [P, S + PAD], F32)
-            nc.gpsimd.memset(t[:, S:], 0.0)
-            y.append(t)
 
         xg, xsg = {}, {}
 

@@ -13,8 +13,8 @@ BANK = 512
 PAIR = 2
 TURNED = 2
 FULLEST = 0
-A_BANKS = (0, 2, 4, 6, 0, 4)
-B_BANKS = (1, 3, 5, 7, 2, 6)
+A_BANKS = (0, 1, 3, 5, 7, 1)
+B_BANKS = (2, 4, 6, 0, 2, 3)
 
 F32 = mybir.dt.float32
 BF16 = mybir.dt.bfloat16
@@ -51,8 +51,8 @@ def tile_moe_ecr_glu_gelu_kernel(tc, x_words, x_scales, w1_words, w1_scales, w3_
             return plane
 
         xs = zero_plane("xs", T)
-        w3s = zero_plane("w3s", E * H)
-        w1s = zero_plane("w1s", E * H + 4)
+        w1s = zero_plane("w1s", E * H)
+        w3s = zero_plane("w3s", E * H + 4)
         w2s = zero_plane("w2s", E * N + 4)
         ident = sb("ident", [P, P], F32)
         nc.vector.memset(ident[:], 0.0)
@@ -84,8 +84,9 @@ def tile_moe_ecr_glu_gelu_kernel(tc, x_words, x_scales, w1_words, w1_scales, w3_
         offs_sb = load_list("offs_sb", offs)
         for r in range(4):
             load_row(xs, x_scales, r)
-        for r in range(4):
+        for r in range(3):
             load_row(w1s, w1_rows, r)
+        load_row(w1s, w1_rows, 3, nc.gpsimd)
         for r in (2, 3):
             load_row(w3s, w3_rows, r, nc.gpsimd)
         make_identity(nc, ident[:], nomemset=True)
@@ -137,6 +138,12 @@ def tile_moe_ecr_glu_gelu_kernel(tc, x_words, x_scales, w1_words, w1_scales, w3_
                 stop=True,
             )
 
+        def by_half(t):
+            return t[:].rearrange("p (m u v) -> p u m v", u=2, v=2)
+
+        def in_order(t):
+            return t[:].rearrange("p (u m v) -> p u m v", u=2, v=2)
+
         def linear_side(e):
             b_ps[e] = bank(B_BANKS[e], "b%d" % e)
             first_pass(b_ps[e], w3w, w3s, e)
@@ -146,11 +153,11 @@ def tile_moe_ecr_glu_gelu_kernel(tc, x_words, x_scales, w1_words, w1_scales, w3_
             first_pass(a_ps[e], w1w, w1s, e)
             tag = "shared" if e == E - 1 else "act%d" % e
             act[e] = keep.tile([P, H], F32, name="act%d" % e, tag=tag, align_bytes=64)
-            nc.scalar.activation(act[e][:], a_ps[e][:], GELU)
+            nc.scalar.activation(in_order(act[e]), by_half(a_ps[e]), GELU)
 
         def product(e):
             hh[e] = keep.tile([P, H], BF16, name="h%d" % e, tag="h%d" % e, align_bytes=64)
-            nc.vector.tensor_tensor(hh[e][:], b_ps[e][:], act[e][:], MULT)
+            nc.vector.tensor_tensor(in_order(hh[e]), by_half(b_ps[e]), in_order(act[e]), MULT)
 
         def turn(e0, e1, b, move=nc.scalar.copy):
             turned = bank(b, "turned%d" % e0)
@@ -158,7 +165,7 @@ def tile_moe_ecr_glu_gelu_kernel(tc, x_words, x_scales, w1_words, w1_scales, w3_
                 pairs = hh[e][:].bitcast(F32)
                 for u in range(2):
                     at = (2 * (e - e0) + u) * P
-                    nc.tensor.transpose(turned[:, at : at + P], pairs[:, u : 2 * P : 2], ident[:])
+                    nc.tensor.transpose(turned[:, at : at + P], pairs[:, u * P : (u + 1) * P], ident[:])
             move(
                 ht[:, e0 * 4 * C : e1 * 4 * C].bitcast(F32).rearrange("p (e s u) -> p e s u", e=e1 - e0, u=2),
                 turned[:, 0 : 2 * P * (e1 - e0)].rearrange("p (e u s) -> p e s u", e=e1 - e0, u=2),
@@ -183,10 +190,11 @@ def tile_moe_ecr_glu_gelu_kernel(tc, x_words, x_scales, w1_words, w1_scales, w3_
                 stop=True,
             )
 
-        for e0 in range(0, E, PAIR):
-            for side in (gated_side, linear_side):
-                for e in range(e0, e0 + PAIR):
-                    side(e)
+        gated_side(0)
+        for e in range(E):
+            if e + 1 < E:
+                gated_side(e + 1)
+            linear_side(e)
         for e in range(E):
             product(e)
         turn(0, 2, A_BANKS[4])
@@ -205,10 +213,10 @@ def tile_moe_ecr_glu_gelu_kernel(tc, x_words, x_scales, w1_words, w1_scales, w3_
                 second_layer(y_ps[:, (e - e0) * C : (e - e0 + 1) * C], e, nb)
             move(y[nb][:, e0 * C : e1 * C], y_ps[:, 0 : (e1 - e0) * C])
 
-        results(0, 0, 2, 7)
-        results(0, 2, 4, 4)
+        results(0, 0, 2, 0)
+        results(0, 2, 4, 1)
         results(0, 4, 5, 2, nc.vector.tensor_copy)
-        results(0, 5, 6, 6)
+        results(0, 5, 6, 3)
         first = TURNED * P
         picked = {}
 
@@ -217,11 +225,11 @@ def tile_moe_ecr_glu_gelu_kernel(tc, x_words, x_scales, w1_words, w1_scales, w3_
             nc.scalar.activation(t[:], y[nb][:].indirect(pos[r][:, t0 // 16 :]), COPY)
             picked[nb, r] = (t, t0)
 
-        results(1, 0, 4, 3)
-        results(1, 4, 6, 5)
+        results(1, 0, 4, 4)
+        results(1, 4, 6, 6)
         pick(0, 0, 0)
-        results(2, 0, 4, 7)
-        results(2, 4, 6, 4)
+        results(2, 0, 4, 0)
+        results(2, 4, 6, 1)
         pick(1, 0, 0)
         pick(2, 0, 0)
 
@@ -262,17 +270,17 @@ def tile_moe_ecr_glu_gelu_kernel(tc, x_words, x_scales, w1_words, w1_scales, w3_
             nc.scalar.copy(res[:], back[:, 0:width])
             queue.dma_start(out[nb * P : (nb + 1) * P, tb0 * P : tb0 * P + width], res[:])
 
-        block0 = summed(0, [weighted(0, r, 0, T) for r in (3, 2, 1, 0)], ((0, 4), (4, 5)), (0, 1))
-        block1 = summed(1, [weighted(1, r, 0, T) for r in (3, 2, 1, 0)], ((0, 4), (4, 5)), (2, 3))
-        store(0, 0, block0[:4], 5, nc.sync)
-        store(0, 4, block0[4:], 6, nc.sync)
-        store(1, 0, block1[:4], 7, nc.sync)
+        block0 = summed(0, [weighted(0, r, 0, T) for r in (3, 2, 1, 0)], ((0, 4), (4, 5)), (7, 5))
+        block1 = summed(1, [weighted(1, r, 0, T) for r in (3, 2, 1, 0)], ((0, 4), (4, 5)), (2, 4))
+        store(0, 0, block0[:4], 6, nc.sync)
+        store(0, 4, block0[4:], 3, nc.sync)
+        store(1, 0, block1[:4], 0, nc.sync)
 
         nb = NB - 1
         whole = [weighted(nb, r, 0, T) for r in (0, 3)]
-        block2 = summed(nb, whole + [weighted(nb, r, 0, first) for r in (1, 2)], ((0, 1), (1, 2)), (2, 3))
-        store(1, 4, block1[4:], 4, nc.sync)
-        store(nb, 0, block2, 0, nc.scalar)
+        block2 = summed(nb, whole + [weighted(nb, r, 0, first) for r in (1, 2)], ((0, 1), (1, 2)), (2, 4))
+        store(1, 4, block1[4:], 1, nc.sync)
+        store(nb, 0, block2, 7, nc.scalar)
         partial = added("pair", whole[0][:, first:], whole[1][:, first:])
         third = weighted(nb, 2, first, T)
         pieces = ((first, T - P), (T - P, T))

@@ -51,8 +51,8 @@ def tile_moe_ecr_glu_gelu_kernel(tc, x_words, x_scales, w1_words, w1_scales, w3_
             return plane
 
         xs = zero_plane("xs", T)
-        w1s = zero_plane("w1s", E * H)
-        w3s = zero_plane("w3s", E * H + 4)
+        w3s = zero_plane("w3s", E * H)
+        w1s = zero_plane("w1s", E * H + 4)
         w2s = zero_plane("w2s", E * N + 4)
         ident = sb("ident", [P, P], F32)
         nc.vector.memset(ident[:], 0.0)
@@ -84,9 +84,8 @@ def tile_moe_ecr_glu_gelu_kernel(tc, x_words, x_scales, w1_words, w1_scales, w3_
         offs_sb = load_list("offs_sb", offs)
         for r in range(4):
             load_row(xs, x_scales, r)
-        for r in range(3):
+        for r in range(4):
             load_row(w1s, w1_rows, r)
-        load_row(w1s, w1_rows, 3, nc.gpsimd)
         for r in (2, 3):
             load_row(w3s, w3_rows, r, nc.gpsimd)
         make_identity(nc, ident[:], nomemset=True)

@@ -219,8 +219,8 @@ def tile_moe_ecr_glu_gelu_kernel(tc, x_words, x_scales, w1_words, w1_scales, w3_
         first = TURNED * P
         picked = {}
 
-        def pick(nb, r, t0):
-            t = sb("picked%d_%d" % (nb, r), [P, T - t0], F32)
+        def pick(nb, r, t0, tag=None):
+            t = keep.tile([P, T - t0], F32, name="picked%d_%d" % (nb, r), tag=tag or "picked%d" % nb, align_bytes=64)
             nc.scalar.activation(t[:], y[nb][:].indirect(pos[r][:, t0 // 16 :]), COPY)
             picked[nb, r] = (t, t0)
 
@@ -230,14 +230,17 @@ def tile_moe_ecr_glu_gelu_kernel(tc, x_words, x_scales, w1_words, w1_scales, w3_
         results(2, 0, 4, 0)
         results(2, 4, 6, 1)
         pick(1, 0, 0)
-        pick(2, 0, 0)
 
         def weighted(nb, r, t0, t1):
-            prod = sb("prod%d_%d_%d" % (nb, r, t0), [P, t1 - t0], F32)
+            name = "prod%d_%d_%d" % (nb, r, t0)
+            prod = keep.tile([P, t1 - t0], F32, name=name, tag=name, align_bytes=64)
             t, at = picked.get((nb, r), (None, T))
             values = t[:, t0 - at : t1 - at] if t0 >= at else y[nb][:].indirect(pos[r][:, t0 // 16 : t1 // 16])
             nc.vector.tensor_tensor(prod[:], values, gates[r][:, t0:t1], MULT)
             return prod
+
+        def tiles(prod):
+            return [prod[:, at : at + P] for at in range(0, prod.shape[1], P)]
 
         def added(name, a, b):
             res = sb(name, list(a.shape), F32)
@@ -250,7 +253,7 @@ def tile_moe_ecr_glu_gelu_kernel(tc, x_words, x_scales, w1_words, w1_scales, w3_
                 for (g0, g1), acc in zip(groups, sums):
                     for tb in range(g0, g1):
                         nc.tensor.matmul(
-                            acc[:, (tb - g0) * P : (tb - g0 + 1) * P], prod[:, tb * P : (tb + 1) * P], ident[:],
+                            acc[:, (tb - g0) * P : (tb - g0 + 1) * P], prod[tb], ident[:],
                             start=(i == 0 and tb == g0), stop=(i == TOP - 1 and tb == g1 - 1), is_transpose=True,
                         )
             by_token = []
@@ -269,15 +272,18 @@ def tile_moe_ecr_glu_gelu_kernel(tc, x_words, x_scales, w1_words, w1_scales, w3_
             nc.scalar.copy(res[:], back[:, 0:width])
             queue.dma_start(out[nb * P : (nb + 1) * P, tb0 * P : tb0 * P + width], res[:])
 
-        block0 = summed(0, [weighted(0, r, 0, T) for r in (3, 2, 1, 0)], ((0, 4), (4, 5)), (7, 5))
-        block1 = summed(1, [weighted(1, r, 0, T) for r in (3, 2, 1, 0)], ((0, 4), (4, 5)), (2, 4))
+        opening = tiles(weighted(0, 3, 0, first)) + tiles(weighted(0, 3, first, T))
+        block0 = summed(0, [opening] + [tiles(weighted(0, r, 0, T)) for r in (2, 1, 0)], ((0, 4), (4, 5)), (7, 5))
+        pick(2, 0, 0, "prod0_0_0")
+        block1 = summed(1, [tiles(weighted(1, r, 0, T)) for r in (3, 2, 1, 0)], ((0, 4), (4, 5)), (2, 4))
         store(0, 0, block0[:4], 6, nc.sync)
         store(0, 4, block0[4:], 3, nc.sync)
         store(1, 0, block1[:4], 0, nc.sync)
 
         nb = NB - 1
-        whole = [weighted(nb, r, 0, T) for r in (0, 3)]
-        block2 = summed(nb, whole + [weighted(nb, r, 0, first) for r in (1, 2)], ((0, 1), (1, 2)), (2, 4))
+        whole = [weighted(nb, r, 0, T) for r in (3, 0)]
+        terms = [tiles(t) for t in whole + [weighted(nb, r, 0, first) for r in (1, 2)]]
+        block2 = summed(nb, terms, ((0, 1), (1, 2)), (2, 4))
         store(1, 4, block1[4:], 1, nc.sync)
         store(nb, 0, block2, 7, nc.scalar)
         partial = added("pair", whole[0][:, first:], whole[1][:, first:])

@@ -52,15 +52,21 @@ def tile_moe_ecr_glu_gelu_kernel(tc, x_words, x_scales, w1_words, w1_scales, w3_
 
         xs = zero_plane("xs", T)
         w3s = zero_plane("w3s", E * H)
+        zeros = sb("zeros", [P, PAD], I32)
+        nc.vector.memset(zeros[:], 0)
         w1s = zero_plane("w1s", E * H + 4)
-        w2s = zero_plane("w2s", E * N + 4)
+
+        def clear(words):
+            times = words.shape[1] // PAD
+            nc.scalar.copy(words.rearrange("p (a b) -> p a b", a=times), zeros[:].bitcast(U32).unsqueeze(1).to_broadcast([P, times, PAD]))
+
+        y = [sb("y%d" % nb, [P, S + PAD], F32) for nb in range(NB)]
+        for t in y:
+            nc.scalar.activation(t[:, S:], zeros[:].bitcast(F32), GELU)
         ident = sb("ident", [P, P], F32)
-        nc.vector.memset(ident[:], 0.0)
-        y = []
-        for nb in range(NB):
-            t = sb("y%d" % nb, [P, S + PAD], F32)
-            nc.vector.memset(t[:, S:], 0.0)
-            y.append(t)
+        clear(ident[:].bitcast(U32))
+        w2s = sb("w2s", [P, E * N], U8)
+        clear(w2s[:].bitcast(U32))
 
         def load_row(plane, scales, r, queue=nc.sync):
             src = scales.rearrange("e (q r) c -> r q e c", r=4)[r]
@@ -101,7 +107,7 @@ def tile_moe_ecr_glu_gelu_kernel(tc, x_words, x_scales, w1_words, w1_scales, w3_
         for r, lst in ((1, pos2), (0, pos1)):
             pos[r] = load_list("pos_sb%d" % r, lst)
         for r in range(4):
-            load_row(w2s, w2_rows, r)
+            load_row(w2s, w2_rows, r, nc.sync if r < 2 else nc.gpsimd)
         gates = {}
         for r0, r1 in ((2, 4), (1, 2), (0, 1)):
             t = sb("gates%d" % r0, [P, r1 - r0, T], F32)

from contextlib import ExitStack

import concourse.mybir as mybir
from concourse.masks import make_identity

K, T, E, C, H, N = 512, 640, 6, 128, 512, 384
TOP, PAD = 4, 64
S = E * C
P = 128
NB = N // P
TB = T // P
BANK = 512
PAIR = 2
TURNED = 2
FULLEST = 0
A_BANKS = (0, 1, 3, 5, 7, 1)
B_BANKS = (2, 4, 6, 0, 2, 3)

F32 = mybir.dt.float32
BF16 = mybir.dt.bfloat16
I32 = mybir.dt.int32
U32 = mybir.dt.uint32
U16 = mybir.dt.uint16
U8 = mybir.dt.uint8
FP8X4 = mybir.dt.float8_e4m3fn_x4
FP4X4 = mybir.dt.float4_e2m1fn_x4
MULT = mybir.AluOpType.mult
ADD = mybir.AluOpType.add
COPY = mybir.ActivationFunctionType.Copy
GELU = mybir.ActivationFunctionType.Gelu_apprx_tanh

FLOPS = 2 * S * (2 * K * H + H * N)
BYTES = K * T + 16 * T + E * (2 * (K * H // 2 + 16 * H) + H * N // 2 + 16 * N) + 4 * TOP * T + 2 * P * (S + TOP * T) // 16 + 4 * N * T


def tile_moe_ecr_glu_gelu_kernel(tc, x_words, x_scales, w1_words, w1_scales, w3_words, w3_scales, w2_words, w2_scales, gate, offs, pos1, pos2, pos3, pos4, out):
    nc = tc.nc
    with ExitStack() as ctx:
        keep = ctx.enter_context(tc.tile_pool(name="keep", bufs=1))
        psum = ctx.enter_context(tc.psum_pool(name="psum", bufs=1))

        def sb(name, shape, dtype):
            return keep.tile(shape, dtype, name=name, align_bytes=64)

        def bank(b, name):
            return psum.tile([P, BANK], F32, name=name, tag="bank%d" % b)

        def zero_plane(name, width):
            plane = sb(name, [P, width], U8)
            nc.vector.memset(plane[:].bitcast(I32), 0)
            return plane

        xs = zero_plane("xs", T)
        w3s = zero_plane("w3s", E * H)
        zeros = sb("zeros", [P, PAD], I32)
        nc.vector.memset(zeros[:], 0)
        w1s = zero_plane("w1s", E * H + 4)

        def clear(words):
            times = words.shape[1] // PAD
            nc.scalar.copy(words.rearrange("p (a b) -> p a b", a=times), zeros[:].bitcast(U32).unsqueeze(1).to_broadcast([P, times, PAD]))

        y = [sb("y%d" % nb, [P, S + PAD], F32) for nb in range(NB)]
        for t in y:
            nc.scalar.activation(t[:, S:], zeros[:].bitcast(F32), GELU)
        ident = sb("ident", [P, P], F32)
        clear(ident[:].bitcast(U32))
        w2s = sb("w2s", [P, E * N], U8)
        clear(w2s[:].bitcast(U32))

        def load_row(plane, scales, r, queue=nc.sync):
            src = scales.rearrange("e (q r) c -> r q e c", r=4)[r]
            width = scales.shape[0] * scales.shape[2]
            dst = plane[r:P:32, 0:width].bitcast(I32).rearrange("q (e c) -> q e c", e=scales.shape[0])
            queue.dma_start(dst, src.bitcast(I32))

        def load_words(name, words, e0, e1, c0, c1):
            t = sb(name, [P, e1 - e0, c1 - c0], U8)
            nc.sync.dma_start(t[:].bitcast(I32), words.rearrange("e o p c -> p (e o) c")[:, e0:e1, c0:c1].bitcast(I32))
            return t

        def load_list(name, lst):
            t = keep.tile(list(lst.shape), U16, name=name)
            nc.sync.dma_start(t[:], lst)
            return t

        w1_rows, w3_rows, w2_rows = (s.rearrange("e o q c -> (e o) q c") for s in (w1_scales, w3_scales, w2_scales))
        xw = sb("xw", [P, T], I32)
        nc.sync.dma_start(xw[:], x_words[0].rearrange("p t r -> p (t r)").bitcast(I32))
        offs_sb = load_list("offs_sb", offs)
        for r in range(4):
            load_row(xs, x_scales, r)
        for r in range(4):
            load_row(w1s, w1_rows, r)
        for r in (2, 3):
            load_row(w3s, w3_rows, r, nc.gpsimd)
        make_identity(nc, ident[:], nomemset=True)
        w1w = [load_words("w1w0", w1_words, 0, PAIR, 0, 2 * H)]
        w3w = [load_words("w3w0", w3_words, 0, PAIR, 0, 2 * H)]
        for r in (0, 1):
            load_row(w3s, w3_rows, r)
        for g in range(1, E // PAIR):
            w1w.append(load_words("w1w%d" % g, w1_words, PAIR * g, PAIR * (g + 1), 0, 2 * H))
            w3w.append(load_words("w3w%d" % g, w3_words, PAIR * g, PAIR * (g + 1), 0, 2 * H))
        pos = {r: load_list("pos_sb%d" % r, lst) for r, lst in ((3, pos4), (2, pos3))}
        w2w = load_words("w2w", w2_words, 0, E, 0, 2 * N)
        for r, lst in ((1, pos2), (0, pos1)):
            pos[r] = load_list("pos_sb%d" % r, lst)
        for r in range(4):
            load_row(w2s, w2_rows, r, nc.sync if r < 2 else nc.gpsimd)
        gates = {}
        for r0, r1 in ((2, 4), (1, 2), (0, 1)):
            t = sb("gates%d" % r0, [P, r1 - r0, T], F32)
            nc.sync.dma_start(t[:], gate[r0:r1, 0:P, :].rearrange("r p t -> p r t"))
            for r in range(r0, r1):
                gates[r] = t[:, r - r0, :]

        xg, xsg = {}, {}

        def gather(into, name, window, dtype, e0, e1):
            t = sb("%s%d" % (name, e0), [P, (e1 - e0) * C], dtype)
            nc.vector.tensor_copy(t[:], window.indirect(offs_sb[:, e0 * C // 16 : e1 * C // 16]))
            for e in range(e0, e1):
                into[e] = t[:, (e - e0) * C : (e - e0 + 1) * C]

        for e0, e1 in ((0, 3), (3, 6)):
            gather(xg, "xg", xw[:].bitcast(U32), U32, e0, e1)
        for e0, e1 in ((0, 1), (1, 3), (3, 6)):
            gather(xsg, "xsg", xs[:], U8, e0, e1)

        a_ps, b_ps, act, hh, hq, hs = {}, {}, {}, {}, {}, {}
        ht = sb("ht", [P, E * 4 * C], BF16)

        def first_pass(dst, words, plane, e):
            g, j = divmod(e, PAIR)
            nc.tensor.matmul_mx(
                dst[:],
                lhsT=xg[e].bitcast(FP8X4),
                lhsT_scale=xsg[e],
                rhs=words[g][:, j, :].bitcast(FP4X4),
                rhs_scale=plane[:, e * H : (e + 1) * H],
                start=True,
                stop=True,
            )

        def by_half(t):
            return t[:].rearrange("p (m u v) -> p u m v", u=2, v=2)

        def in_order(t):
            return t[:].rearrange("p (u m v) -> p u m v", u=2, v=2)

        def linear_side(e):
            b_ps[e] = bank(B_BANKS[e], "b%d" % e)
            first_pass(b_ps[e], w3w, w3s, e)

        def gated_side(e):
            a_ps[e] = bank(A_BANKS[e], "a%d" % e)
            first_pass(a_ps[e], w1w, w1s, e)
            tag = "shared" if e == E - 1 else "act%d" % e
            act[e] = keep.tile([P, H], F32, name="act%d" % e, tag=tag, align_bytes=64)
            nc.scalar.activation(in_order(act[e]), by_half(a_ps[e]), GELU)

        def product(e):
            hh[e] = keep.tile([P, H], BF16, name="h%d" % e, tag="h%d" % e, align_bytes=64)
            nc.vector.tensor_tensor(in_order(hh[e]), by_half(b_ps[e]), in_order(act[e]), MULT)

        def turn(e0, e1, b, move=nc.scalar.copy):
            turned = bank(b, "turned%d" % e0)
            for e in range(e0, e1):
                pairs = hh[e][:].bitcast(F32)
                for u in range(2):
                    at = (2 * (e - e0) + u) * P
                    nc.tensor.transpose(turned[:, at : at + P], pairs[:, u * P : (u + 1) * P], ident[:])
            move(
                ht[:, e0 * 4 * C : e1 * 4 * C].bitcast(F32).rearrange("p (e s u) -> p e s u", e=e1 - e0, u=2),
                turned[:, 0 : 2 * P * (e1 - e0)].rearrange("p (e u s) -> p e s u", e=e1 - e0, u=2),
            )

        def quantise(e0, e1, tag):
            codes = keep.tile([P, (e1 - e0) * C], U32, name="hq%d" % e0, tag=tag, align_bytes=64)
            plane = sb("hs%d" % e0, [P, (e1 - e0) * C], U8)
            nc.vector.quantize_mx(codes[:].bitcast(FP8X4), plane[:], ht[:, e0 * 4 * C : e1 * 4 * C])
            for e in range(e0, e1):
                hq[e] = codes[:, (e - e0) * C : (e - e0 + 1) * C]
                hs[e] = plane[:, (e - e0) * C : (e - e0 + 1) * C]

        def second_layer(dst, e, nb):
            nc.tensor.matmul_mx(
                dst,
                lhsT=w2w[:, e, 2 * P * nb : 2 * P * (nb + 1)].bitcast(FP4X4),
                lhsT_scale=w2s[:, e * N + P * nb : e * N + P * (nb + 1)],
                rhs=hq[e].bitcast(FP8X4),
                rhs_scale=hs[e],
                start=True,
                stop=True,
            )

        gated_side(0)
        for e in range(E):
            if e + 1 < E:
                gated_side(e + 1)
            linear_side(e)
        for e in range(E):
            product(e)
        turn(0, 2, A_BANKS[4])
        turn(2, 3, A_BANKS[5])
        turn(3, 4, B_BANKS[4], nc.vector.tensor_copy)
        turn(4, 5, B_BANKS[1])
        turn(5, 6, B_BANKS[2])
        quantise(0, 2, "shared")
        quantise(2, 4, "hq2")
        quantise(4, 5, "hq4")
        quantise(5, 6, "hq5")

        def results(nb, e0, e1, b, move=nc.scalar.copy):
            y_ps = bank(b, "y%d_%d" % (nb, e0))
            for e in range(e0, e1):
                second_layer(y_ps[:, (e - e0) * C : (e - e0 + 1) * C], e, nb)
            move(y[nb][:, e0 * C : e1 * C], y_ps[:, 0 : (e1 - e0) * C])

        results(0, 0, 2, 0)
        results(0, 2, 4, 1)
        results(0, 4, 5, 2, nc.vector.tensor_copy)
        results(0, 5, 6, 3)
        first = TURNED * P
        picked = {}

        def pick(nb, r, t0, tag=None):
            t = keep.tile([P, T - t0], F32, name="picked%d_%d" % (nb, r), tag=tag or "picked%d" % nb, align_bytes=64)
            nc.scalar.activation(t[:], y[nb][:].indirect(pos[r][:, t0 // 16 :]), COPY)
            picked[nb, r] = (t, t0)

        results(1, 0, 4, 4)
        results(1, 4, 6, 6)
        pick(0, 0, 0)
        results(2, 0, 4, 0)
        results(2, 4, 6, 1)
        pick(1, 0, 0)

        def weighted(nb, r, t0, t1):
            name = "prod%d_%d_%d" % (nb, r, t0)
            prod = keep.tile([P, t1 - t0], F32, name=name, tag=name, align_bytes=64)
            t, at = picked.get((nb, r), (None, T))
            values = t[:, t0 - at : t1 - at] if t0 >= at else y[nb][:].indirect(pos[r][:, t0 // 16 : t1 // 16])
            nc.vector.tensor_tensor(prod[:], values, gates[r][:, t0:t1], MULT)
            return prod

        def tiles(prod):
            return [prod[:, at : at + P] for at in range(0, prod.shape[1], P)]

        def added(name, a, b):
            res = sb(name, list(a.shape), F32)
            nc.vector.tensor_tensor(res[:], a, b, ADD)
            return res

        def summed(nb, prods, groups, banks):
            sums = [bank(b, "sum%d_%d" % (nb, g0)) for (g0, g1), b in zip(groups, banks)]
            for i, prod in enumerate(prods):
                for (g0, g1), acc in zip(groups, sums):
                    for tb in range(g0, g1):
                        nc.tensor.matmul(
                            acc[:, (tb - g0) * P : (tb - g0 + 1) * P], prod[tb], ident[:],
                            start=(i == 0 and tb == g0), stop=(i == TOP - 1 and tb == g1 - 1), is_transpose=True,
                        )
            by_token = []
            for (g0, g1), acc in zip(groups, sums):
                t = sb("z%d_%d" % (nb, g0), [P, (g1 - g0) * P], F32)
                nc.scalar.copy(t[:], acc[:, 0 : (g1 - g0) * P])
                by_token.extend(t[:, at : at + P] for at in range(0, (g1 - g0) * P, P))
            return by_token

        def store(nb, tb0, by_token, b, queue):
            width = len(by_token) * P
            back = bank(b, "back%d_%d" % (nb, tb0))
            for i, t in enumerate(by_token):
                nc.tensor.transpose(back[:, i * P : (i + 1) * P], t, ident[:])
            res = sb("res%d_%d" % (nb, tb0), [P, width], F32)
            nc.scalar.copy(res[:], back[:, 0:width])
            queue.dma_start(out[nb * P : (nb + 1) * P, tb0 * P : tb0 * P + width], res[:])

        opening = tiles(weighted(0, 3, 0, first)) + tiles(weighted(0, 3, first, T))
        block0 = summed(0, [opening] + [tiles(weighted(0, r, 0, T)) for r in (2, 1, 0)], ((0, 4), (4, 5)), (7, 5))
        pick(2, 0, 0, "prod0_0_0")
        block1 = summed(1, [tiles(weighted(1, r, 0, T)) for r in (3, 2, 1, 0)], ((0, 4), (4, 5)), (2, 4))
        store(0, 0, block0[:4], 6, nc.sync)
        store(0, 4, block0[4:], 3, nc.sync)
        store(1, 0, block1[:4], 0, nc.sync)

        nb = NB - 1
        whole = [weighted(nb, r, 0, T) for r in (3, 0)]
        terms = [tiles(t) for t in whole + [weighted(nb, r, 0, first) for r in (1, 2)]]
        block2 = summed(nb, terms, ((0, 1), (1, 2)), (2, 4))
        store(1, 4, block1[4:], 1, nc.sync)
        store(nb, 0, block2, 7, nc.scalar)
        partial = added("pair", whole[0][:, first:], whole[1][:, first:])
        third = weighted(nb, 2, first, T)
        pieces = ((first, T - P), (T - P, T))
        last = [weighted(nb, 1, *pieces[0])]
        partial = added("triple", partial[:], third[:])
        last.append(weighted(nb, 1, *pieces[1]))
        for (t0, t1), term in zip(pieces, last):
            res = added("end%d" % t0, partial[:, t0 - first : t1 - first], term[:])
            nc.sync.dma_start(out[nb * P : (nb + 1) * P, t0:t1], res[:])
